import numpy as np
import ml_dtypes


def mxq(x, axis, fmt="e4m3"):
    dtype, down = {"e4m3": (ml_dtypes.float8_e4m3fn, 7), "e5m2": (ml_dtypes.float8_e5m2, 14)}[fmt]
    v = np.moveaxis(np.asarray(x, np.float32).astype(ml_dtypes.bfloat16).astype(np.float64), axis, -1)
    blocks = v.reshape(v.shape[:-1] + (-1, 32))
    amax = np.abs(blocks).max(-1, keepdims=True)
    byte = np.maximum(np.where(amax > 0, np.frexp(amax)[1] - 1 + 127, 0) - down, 1)
    scale = np.exp2(byte - 127.0)
    codes = (blocks / scale).astype(np.float32).astype(dtype).astype(np.float64)
    return np.moveaxis((codes * scale).reshape(v.shape), -1, axis)


WIDE = False


def mx_kscale(k):
    if not WIDE:
        return np.ones(k)
    levels = np.array([10, -10, 5, -5, 0])
    if k % 512:
        return np.exp2(np.random.permutation(np.resize(levels, k // 32))).repeat(32)
    a = np.empty((k // 512, 16))
    for p in range(k // 512):
        a[p, :8] = np.random.permutation(np.resize(levels, 8))
        for g in range(8):
            far = levels[np.abs(levels - a[p, g]) >= 10]
            a[p, g + 8] = far[np.random.randint(len(far))]
    return np.exp2(a.ravel()).repeat(32)


def f64(x):
    return np.asarray(x).astype(np.float64)


def striped(idx):
    return np.tile(idx.reshape(-1, 16).T, (8, 1)).astype(np.uint16)


def unstriped(offs):
    return offs[:16].T.reshape(-1).astype(np.int64)


E2M1 = np.array([0.0, 0.5, 1.0, 1.5, 2.0, 3.0, 4.0, 6.0, -0.0, -0.5, -1.0, -1.5, -2.0, -3.0, -4.0, -6.0])


def pack_weight(w, fmt):
    k, n = w.shape
    w = f64(np.asarray(w, np.float32).astype(ml_dtypes.bfloat16)).reshape(k // 32, 32, n)
    amax = np.abs(w).max(1)
    if fmt == "e4m3":
        byte = np.frexp(amax)[1] - 1 + 127 - 7
    else:
        mant, ex = np.frexp(amax / 6.0)
        byte = np.where(mant > 0.5, ex, ex - 1) + 127
    byte = np.clip(np.where(amax > 0, byte, 1), 1, 254)
    scaled = (w * np.exp2(127.0 - byte)[:, None, :]).reshape(k, n).astype(np.float32)
    by_word = np.ascontiguousarray(scaled.reshape(k // 512, 128, 4, n).transpose(0, 1, 3, 2))
    if fmt == "e4m3":
        words = by_word.astype(ml_dtypes.float8_e4m3fn).view(np.uint8)
    else:
        c = by_word.astype(ml_dtypes.float4_e2m1fn).view(np.uint8) & 0xF
        words = (c[..., 0::2] | (c[..., 1::2] << 4)).reshape(k // 512, 128, 2 * n)
    return np.ascontiguousarray(words), np.ascontiguousarray(byte.astype(np.uint8).reshape(k // 512, 16, n))


def unpack_weight(words, scales, fmt):
    g, _, n = scales.shape
    words = np.ascontiguousarray(words).reshape(g, 128, n, -1)
    if fmt == "e4m3":
        vals = words.view(ml_dtypes.float8_e4m3fn).astype(np.float64)
    else:
        nib = np.empty((g, 128, n, 4), np.uint8)
        nib[..., 0::2] = words & 0xF
        nib[..., 1::2] = words >> 4
        vals = E2M1[nib]
    vals = vals * np.repeat(np.exp2(scales.astype(np.float64) - 127.0), 8, axis=1)[..., None]
    return vals.transpose(0, 1, 3, 2).reshape(g * 512, n)


def gelu(v):
    return 0.5 * v * (1.0 + np.tanh(np.sqrt(2.0 / np.pi) * (v + 0.044715 * v**3)))


K, T, Q, E, C, D, H = 1024, 1024, 1024, 4, 128, 128, 0
N = 128


def by_expert(wq, xq, C):
    return np.concatenate([wq[e].T @ xq[:, e * C:(e + 1) * C] for e in range(E)], axis=1)


def setup_inputs():
    n = np.random.standard_normal
    s = mx_kscale(K)
    slot_token = np.random.permutation(T)[:E * C]
    slots2 = np.concatenate([np.random.permutation(Q)[:D] for e in range(E)])
    x = pack_weight(n((K, Q)) * s[:, None], "e4m3")
    w = [pack_weight(m, "e2m1") for m in n((E, K, N)) / np.sqrt(K) / s[None, :, None]]
    return {
        "x_words": x[0],
        "x_scales": x[1],
        "xo": (n((K, T)) * s[:, None]).astype(np.float32),
        "w_words": np.stack([m[0] for m in w]),
        "w_scales": np.stack([m[1] for m in w]),
        "gate": np.tile(np.random.uniform(0.2, 1.0, E * C), (128, 1)).astype(np.float32),
        "offs": striped(slot_token),
        "offs2": striped(slots2),
    }


def reference(x_words, x_scales, xo, w_words, w_scales, gate, offs, offs2):
    w = np.stack([unpack_weight(w_words[e], w_scales[e], "e2m1") for e in range(E)])
    idx, idx2 = unstriped(offs), unstriped(offs2)
    xq = mxq(f64(xo)[:, idx], 0, "e4m3")
    rq = unpack_weight(x_words, x_scales, "e4m3")[:, idx2]
    y = gelu(by_expert(w, xq, C))
    z = gelu(by_expert(w, rq, D))
    own = np.zeros((N, T))
    own[:, idx] = f64(gate[:1]) * y
    return np.concatenate([own, z], axis=1)

@@ -1,0 +1,181 @@
+from contextlib import ExitStack
+
+import concourse.mybir as mybir
+
+K, T, Q, E, C, N = 1024, 1024, 1024, 4, 128, 128
+P = 128
+PASSES = 2
+SLOTS = E * C
+LIST_COLS = SLOTS // 16
+COLS_PER_EXPERT = C // 16
+
+FLOPS = 2 * K * N * 2 * SLOTS
+
+F32 = mybir.dt.float32
+BF16 = mybir.dt.bfloat16
+I32 = mybir.dt.int32
+U32 = mybir.dt.uint32
+U16 = mybir.dt.uint16
+U8 = mybir.dt.uint8
+FP8X4 = mybir.dt.float8_e4m3fn_x4
+FP4X4 = mybir.dt.float4_e2m1fn_x4
+GELU = mybir.ActivationFunctionType.Gelu_apprx_tanh
+MULT = mybir.AluOpType.mult
+
+CHUNKS = [
+    [(0, 512, "s"), (512, 1024, "s")],
+    [(0, 512, "s"), (512, 1024, "s")],
+    [(0, 512, "s"), (512, 1024, "s")],
+    [(0, 512, "s"), (512, 768, "s"), (768, 1024, "v")],
+]
+
+
+def tile_moe_loc_lin_gelu_kernel(tc, x_words, x_scales, xo, w_words, w_scales, gate, offs, offs2, out):
+    nc = tc.nc
+    with ExitStack() as ctx:
+        keep = ctx.enter_context(tc.tile_pool(name="keep", bufs=1))
+        psum = ctx.enter_context(tc.psum_pool(name="psum", bufs=1))
+
+        def sbuf(name, shape, dtype):
+            return keep.tile(shape, dtype, name=name, align_bytes=64)
+
+        own_list = keep.tile([P, LIST_COLS], U16, name="own_list")
+        far_list = keep.tile([P, LIST_COLS], U16, name="far_list")
+        far_scale_rows = sbuf("far_scale_rows", [P, PASSES, Q], U8)
+        w_scale_rows = sbuf("w_scale_rows", [P, E * PASSES, N], U8)
+        w_codes = sbuf("w_codes", [P, E * PASSES, 2 * N], U8)
+        far_words = [sbuf(f"far_words{s}", [P, Q], I32) for s in range(PASSES)]
+        far_codes = sbuf("far_codes", [P, PASSES, SLOTS], U32)
+        far_scales = sbuf("far_scales", [P, PASSES, SLOTS], U8)
+        pairs = [sbuf(f"pairs{i}", [P, T, 2], BF16) for i in range(4)]
+        picked = [sbuf(f"picked{s}", [P, 2, 2 * SLOTS], BF16) for s in range(PASSES)]
+        grouped = [sbuf(f"grouped{s}", [P, SLOTS, 2, 2], BF16) for s in range(PASSES)]
+        own_codes = sbuf("own_codes", [P, PASSES, SLOTS], U32)
+        own_scales = sbuf("own_scales", [P, PASSES, SLOTS], U8)
+        gate_sb = sbuf("gate_sb", [P, SLOTS], F32)
+        y_sb = sbuf("y_sb", [P, SLOTS], F32)
+        z_sb = sbuf("z_sb", [P, SLOTS], F32)
+        own = sbuf("own", [P, T], F32)
+        warm_in = sbuf("warm_in", [P, 8], F32)
+        warm_out = sbuf("warm_out", [P, 8], F32)
+        y_banks = [psum.tile([P, C], F32, name=f"y_bank{e}") for e in range(E)]
+        z_bank = psum.tile([P, SLOTS], F32, name="z_bank")
+
+        xo_pairs = xo.rearrange("(s p u e) t -> s u p e t", s=PASSES, p=P, u=2, e=2)
+
+        def load_chunk(i, c0, c1):
+            raw = sbuf(f"raw{i}_{c0}", [P, 2, c1 - c0], F32)
+            nc.sync.dma_start(out=raw[:], in_=xo_pairs[i // 2][i % 2][:, :, c0:c1])
+            return raw
+
+        def cast_chunk(i, c0, c1, eng, raw):
+            src = raw[:].rearrange("p e c -> p c e")
+            if eng == "s":
+                nc.scalar.copy(pairs[i][:, c0:c1, :], src)
+            else:
+                nc.vector.tensor_copy(pairs[i][:, c0:c1, :], src)
+
+        def load_pair(i, first=0, last=None):
+            for c0, c1, eng in CHUNKS[i][first:last]:
+                cast_chunk(i, c0, c1, eng, load_chunk(i, c0, c1))
+
+        def gather_pair(i, e0, e1):
+            window = pairs[i][:].rearrange("p c e -> p (c e)").bitcast(U32)
+            nc.vector.tensor_copy(
+                picked[i // 2][:, i % 2, 2 * C * e0 : 2 * C * e1].bitcast(U32),
+                window.indirect(own_list[:, COLS_PER_EXPERT * e0 : COLS_PER_EXPERT * e1]),
+            )
+
+        def interleave(s, e0, e1):
+            nc.vector.tensor_copy(
+                grouped[s][:, C * e0 : C * e1, :, :].rearrange("p c u e -> p c (u e)").bitcast(F32),
+                picked[s][:, :, 2 * C * e0 : 2 * C * e1].bitcast(F32).rearrange("p u c -> p c u"),
+            )
+
+        def quantise(s, e0, e1):
+            nc.vector.quantize_mx(
+                out=own_codes[:, s, C * e0 : C * e1].bitcast(FP8X4),
+                scales=own_scales[:, s, C * e0 : C * e1],
+                in_=grouped[s][:, C * e0 : C * e1, :, :].rearrange("p c u e -> p (c u e)"),
+            )
+
+        def expert_pass(bank, codes, scales, e, s):
+            nc.tensor.matmul_mx(
+                out=bank,
+                lhsT=w_codes[:, PASSES * e + s, :].bitcast(FP4X4),
+                lhsT_scale=w_scale_rows[:, PASSES * e + s, :],
+                rhs=codes[:, s, C * e : C * (e + 1)].bitcast(FP8X4),
+                rhs_scale=scales[:, s, C * e : C * (e + 1)],
+                start=(s == 0),
+                stop=(s == PASSES - 1),
+            )
+
+        def load_far_words(s):
+            nc.sync.dma_start(out=far_words[s][:], in_=x_words[s].rearrange("p t d -> p (t d)").bitcast(I32))
+
+        def gather_far_words(s):
+            nc.vector.tensor_copy(far_codes[:, s, :], far_words[s][:].bitcast(U32).indirect(far_list[:]))
+
+        nc.gpsimd.memset(far_scale_rows[:].rearrange("p s t -> p (s t)").bitcast(I32), 0)
+        nc.gpsimd.memset(w_scale_rows[:].rearrange("p g n -> p (g n)").bitcast(I32), 0)
+        nc.vector.memset(warm_in[:], 0.0)
+        nc.scalar.activation(warm_out[:], warm_in[:], GELU)
+        nc.gpsimd.memset(own[:], 0.0)
+
+        nc.sync.dma_start(far_list[:], offs2)
+        load_pair(0, 0, 1)
+        x_rows = x_scales.rearrange("s (q r) t -> r q s t", r=4)
+        for r in range(4):
+            nc.sync.dma_start(out=far_scale_rows[r:P:32, :, :].bitcast(I32), in_=x_rows[r].bitcast(I32))
+        for s in range(PASSES):
+            nc.vector.tensor_copy(far_scales[:, s, :], far_scale_rows[:, s, :].indirect(far_list[:]))
+
+        nc.sync.dma_start(own_list[:], offs)
+        load_pair(0, 1)
+        gather_pair(0, 0, E)
+        load_far_words(0)
+        gather_far_words(0)
+        load_pair(1)
+        gather_pair(1, 0, E)
+        interleave(0, 0, E)
+        load_pair(2)
+        quantise(0, 0, E)
+        gather_pair(2, 0, E)
+        load_far_words(1)
+        gather_far_words(1)
+        load_pair(3)
+        w_rows = w_scales.rearrange("e s (q r) n -> r q (e s) n", r=4)
+        for r in range(4):
+            nc.sync.dma_start(out=w_scale_rows[r:P:32, :, :].bitcast(I32), in_=w_rows[r].bitcast(I32))
+        nc.sync.dma_start(out=w_codes[:].bitcast(I32), in_=w_words.rearrange("e s p b -> p (e s) b").bitcast(I32))
+        nc.sync.dma_start(out=gate_sb[:], in_=gate)
+
+        def finish(e):
+            for s in range(PASSES):
+                expert_pass(y_banks[e][:], own_codes, own_scales, e, s)
+            nc.scalar.activation(y_sb[:, C * e : C * (e + 1)], y_banks[e][:], GELU)
+
+        def scatter(e):
+            nc.vector.tensor_tensor(
+                own[:].indirect(own_list[:, COLS_PER_EXPERT * e : COLS_PER_EXPERT * (e + 1)]),
+                y_sb[:, C * e : C * (e + 1)],
+                gate_sb[:, C * e : C * (e + 1)],
+                MULT,
+            )
+
+        for step in range(E + 2):
+            if step < E:
+                gather_pair(3, step, step + 1)
+            if 2 <= step:
+                quantise(1, step - 2, step - 1)
+                finish(step - 2)
+            if 1 <= step <= E:
+                interleave(1, step - 1, step)
+        for e in range(E):
+            for s in range(PASSES):
+                expert_pass(z_bank[:, C * e : C * (e + 1)], far_codes, far_scales, e, s)
+        nc.scalar.activation(z_sb[:], z_bank[:], GELU)
+        nc.scalar.dma_start(out=out[:, T:], in_=z_sb[:])
+        for e in range(E):
+            scatter(e)
+        nc.sync.dma_start(out=out[:, :T], in_=own[:])

@@ -22,9 +22,15 @@ FP4X4 = mybir.dt.float4_e2m1fn_x4
 GELU = mybir.ActivationFunctionType.Gelu_apprx_tanh
 MULT = mybir.AluOpType.mult
 
-CHUNKS = [
+LOADS = [
+    [(0, 512), (512, 1024)],
+    [(0, 1024)],
+    [(0, 512), (512, 1024)],
+    [(0, 512), (512, 1024)],
+]
+CASTS = [
     [(0, 512, "s"), (512, 1024, "s")],
-    [(0, 512, "s"), (512, 1024, "s")],
+    [(0, 480, "s"), (480, 1024, "v")],
     [(0, 512, "s"), (512, 1024, "s")],
     [(0, 512, "s"), (512, 768, "s"), (768, 1024, "v")],
 ]
@@ -58,26 +64,22 @@ def tile_moe_loc_lin_gelu_kernel(tc, x_words, x_scales, xo, w_words, w_scales, g
         own = sbuf("own", [P, T], F32)
         warm_in = sbuf("warm_in", [P, 8], F32)
         warm_out = sbuf("warm_out", [P, 8], F32)
-        y_banks = [psum.tile([P, C], F32, name=f"y_bank{e}") for e in range(E)]
+        y_banks = [psum.tile([P, 2 * C], F32, name=f"y_bank{h}") for h in range(2)]
         z_bank = psum.tile([P, SLOTS], F32, name="z_bank")
 
         xo_pairs = xo.rearrange("(s p u e) t -> s u p e t", s=PASSES, p=P, u=2, e=2)
 
-        def load_chunk(i, c0, c1):
-            raw = sbuf(f"raw{i}_{c0}", [P, 2, c1 - c0], F32)
-            nc.sync.dma_start(out=raw[:], in_=xo_pairs[i // 2][i % 2][:, :, c0:c1])
-            return raw
-
-        def cast_chunk(i, c0, c1, eng, raw):
-            src = raw[:].rearrange("p e c -> p c e")
-            if eng == "s":
-                nc.scalar.copy(pairs[i][:, c0:c1, :], src)
-            else:
-                nc.vector.tensor_copy(pairs[i][:, c0:c1, :], src)
-
-        def load_pair(i, first=0, last=None):
-            for c0, c1, eng in CHUNKS[i][first:last]:
-                cast_chunk(i, c0, c1, eng, load_chunk(i, c0, c1))
+        def load_pair(i):
+            for c0, c1 in LOADS[i]:
+                raw = sbuf(f"raw{i}_{c0}", [P, 2, c1 - c0], F32)
+                nc.sync.dma_start(out=raw[:], in_=xo_pairs[i // 2][i % 2][:, :, c0:c1])
+                for d0, d1, eng in CASTS[i]:
+                    if c0 <= d0 < c1:
+                        src = raw[:, :, d0 - c0 : d1 - c0].rearrange("p e c -> p c e")
+                        if eng == "s":
+                            nc.scalar.copy(pairs[i][:, d0:d1, :], src)
+                        else:
+                            nc.vector.tensor_copy(pairs[i][:, d0:d1, :], src)
 
         def gather_pair(i, e0, e1):
             window = pairs[i][:].rearrange("p c e -> p (c e)").bitcast(U32)
@@ -116,66 +118,55 @@ def tile_moe_loc_lin_gelu_kernel(tc, x_words, x_scales, xo, w_words, w_scales, g
         def gather_far_words(s):
             nc.vector.tensor_copy(far_codes[:, s, :], far_words[s][:].bitcast(U32).indirect(far_list[:]))
 
-        nc.gpsimd.memset(far_scale_rows[:].rearrange("p s t -> p (s t)").bitcast(I32), 0)
+        nc.vector.memset(far_scale_rows[:, 0, :].bitcast(I32), 0)
+        nc.gpsimd.memset(far_scale_rows[:, 1, :].bitcast(I32), 0)
+        nc.gpsimd.memset(warm_in[:], 0.0)
         nc.gpsimd.memset(w_scale_rows[:].rearrange("p g n -> p (g n)").bitcast(I32), 0)
-        nc.vector.memset(warm_in[:], 0.0)
-        nc.scalar.activation(warm_out[:], warm_in[:], GELU)
         nc.gpsimd.memset(own[:], 0.0)
 
         nc.sync.dma_start(far_list[:], offs2)
-        load_pair(0, 0, 1)
+        load_far_words(0)
+        gather_far_words(0)
+        nc.sync.dma_start(own_list[:], offs)
         x_rows = x_scales.rearrange("s (q r) t -> r q s t", r=4)
         for r in range(4):
             nc.sync.dma_start(out=far_scale_rows[r:P:32, :, :].bitcast(I32), in_=x_rows[r].bitcast(I32))
+        nc.scalar.activation(warm_out[:], warm_in[:], GELU)
         for s in range(PASSES):
             nc.vector.tensor_copy(far_scales[:, s, :], far_scale_rows[:, s, :].indirect(far_list[:]))
 
-        nc.sync.dma_start(own_list[:], offs)
-        load_pair(0, 1)
+        load_pair(0)
         gather_pair(0, 0, E)
-        load_far_words(0)
-        gather_far_words(0)
         load_pair(1)
         gather_pair(1, 0, E)
         interleave(0, 0, E)
         load_pair(2)
         quantise(0, 0, E)
         gather_pair(2, 0, E)
-        load_far_words(1)
-        gather_far_words(1)
         load_pair(3)
         w_rows = w_scales.rearrange("e s (q r) n -> r q (e s) n", r=4)
         for r in range(4):
             nc.sync.dma_start(out=w_scale_rows[r:P:32, :, :].bitcast(I32), in_=w_rows[r].bitcast(I32))
         nc.sync.dma_start(out=w_codes[:].bitcast(I32), in_=w_words.rearrange("e s p b -> p (e s) b").bitcast(I32))
+        load_far_words(1)
         nc.sync.dma_start(out=gate_sb[:], in_=gate)
 
-        def finish(e):
-            for s in range(PASSES):
-                expert_pass(y_banks[e][:], own_codes, own_scales, e, s)
-            nc.scalar.activation(y_sb[:, C * e : C * (e + 1)], y_banks[e][:], GELU)
-
-        def scatter(e):
-            nc.vector.tensor_tensor(
-                own[:].indirect(own_list[:, COLS_PER_EXPERT * e : COLS_PER_EXPERT * (e + 1)]),
-                y_sb[:, C * e : C * (e + 1)],
-                gate_sb[:, C * e : C * (e + 1)],
-                MULT,
-            )
-
-        for step in range(E + 2):
-            if step < E:
-                gather_pair(3, step, step + 1)
-            if 2 <= step:
-                quantise(1, step - 2, step - 1)
-                finish(step - 2)
-            if 1 <= step <= E:
-                interleave(1, step - 1, step)
+        halves = [(0, 2), (2, 4)]
+        for e0, e1 in halves:
+            gather_pair(3, e0, e1)
+        for e0, e1 in halves:
+            interleave(1, e0, e1)
+        for h, (e0, e1) in enumerate(halves):
+            quantise(1, e0, e1)
+            for e in range(e0, e1):
+                for s in range(PASSES):
+                    expert_pass(y_banks[h][:, C * (e - e0) : C * (e - e0 + 1)], own_codes, own_scales, e, s)
+            nc.scalar.activation(y_sb[:, C * e0 : C * e1], y_banks[h][:], GELU)
+        gather_far_words(1)
         for e in range(E):
             for s in range(PASSES):
                 expert_pass(z_bank[:, C * e : C * (e + 1)], far_codes, far_scales, e, s)
         nc.scalar.activation(z_sb[:], z_bank[:], GELU)
         nc.scalar.dma_start(out=out[:, T:], in_=z_sb[:])
-        for e in range(E):
-            scatter(e)
+        nc.vector.tensor_tensor(own[:].indirect(own_list[:]), y_sb[:], gate_sb[:], MULT)
         nc.sync.dma_start(out=out[:, :T], in_=own[:])

@@ -22,17 +22,12 @@ FP4X4 = mybir.dt.float4_e2m1fn_x4
 GELU = mybir.ActivationFunctionType.Gelu_apprx_tanh
 MULT = mybir.AluOpType.mult
 
-LOADS = [
-    [(0, 512), (512, 1024)],
-    [(0, 1024)],
-    [(0, 512), (512, 1024)],
-    [(0, 512), (512, 1024)],
-]
+LOADS = [[(0, 512), (512, 1024)]] * 4
 CASTS = [
-    [(0, 512, "s"), (512, 1024, "s")],
-    [(0, 480, "s"), (480, 1024, "v")],
-    [(0, 512, "s"), (512, 1024, "s")],
     [(0, 512, "s"), (512, 768, "s"), (768, 1024, "v")],
+    [(0, 512, "s"), (512, 800, "s"), (800, 1024, "v")],
+    [(0, 512, "s"), (512, 1024, "s")],
+    [(0, 512, "s"), (512, 800, "s"), (800, 1024, "v")],
 ]
 
 
@@ -47,24 +42,24 @@ def tile_moe_loc_lin_gelu_kernel(tc, x_words, x_scales, xo, w_words, w_scales, g
 
         own_list = keep.tile([P, LIST_COLS], U16, name="own_list")
         far_list = keep.tile([P, LIST_COLS], U16, name="far_list")
-        far_scale_rows = sbuf("far_scale_rows", [P, PASSES, Q], U8)
+        far_scale_rows = sbuf("far_scale_rows", [P, Q], U8)
         w_scale_rows = sbuf("w_scale_rows", [P, E * PASSES, N], U8)
         w_codes = sbuf("w_codes", [P, E * PASSES, 2 * N], U8)
         far_words = [sbuf(f"far_words{s}", [P, Q], I32) for s in range(PASSES)]
         far_codes = sbuf("far_codes", [P, PASSES, SLOTS], U32)
-        far_scales = sbuf("far_scales", [P, PASSES, SLOTS], U8)
+        far_scales = [sbuf(f"far_scales{s}", [P, SLOTS], U8) for s in range(PASSES)]
         pairs = [sbuf(f"pairs{i}", [P, T, 2], BF16) for i in range(4)]
         picked = [sbuf(f"picked{s}", [P, 2, 2 * SLOTS], BF16) for s in range(PASSES)]
         grouped = [sbuf(f"grouped{s}", [P, SLOTS, 2, 2], BF16) for s in range(PASSES)]
         own_codes = sbuf("own_codes", [P, PASSES, SLOTS], U32)
-        own_scales = sbuf("own_scales", [P, PASSES, SLOTS], U8)
+        own_scales = [sbuf(f"own_scales{s}", [P, SLOTS], U8) for s in range(PASSES)]
         gate_sb = sbuf("gate_sb", [P, SLOTS], F32)
         y_sb = sbuf("y_sb", [P, SLOTS], F32)
         z_sb = sbuf("z_sb", [P, SLOTS], F32)
         own = sbuf("own", [P, T], F32)
         warm_in = sbuf("warm_in", [P, 8], F32)
         warm_out = sbuf("warm_out", [P, 8], F32)
-        y_banks = [psum.tile([P, 2 * C], F32, name=f"y_bank{h}") for h in range(2)]
+        y_banks = [psum.tile([P, C], F32, name=f"y_bank{e}") for e in range(E)]
         z_bank = psum.tile([P, SLOTS], F32, name="z_bank")
 
         xo_pairs = xo.rearrange("(s p u e) t -> s u p e t", s=PASSES, p=P, u=2, e=2)
@@ -88,8 +83,8 @@ def tile_moe_loc_lin_gelu_kernel(tc, x_words, x_scales, xo, w_words, w_scales, g
                 window.indirect(own_list[:, COLS_PER_EXPERT * e0 : COLS_PER_EXPERT * e1]),
             )
 
-        def interleave(s, e0, e1):
-            nc.vector.tensor_copy(
+        def interleave(copy, s, e0, e1):
+            copy(
                 grouped[s][:, C * e0 : C * e1, :, :].rearrange("p c u e -> p c (u e)").bitcast(F32),
                 picked[s][:, :, 2 * C * e0 : 2 * C * e1].bitcast(F32).rearrange("p u c -> p c u"),
             )
@@ -97,7 +92,7 @@ def tile_moe_loc_lin_gelu_kernel(tc, x_words, x_scales, xo, w_words, w_scales, g
         def quantise(s, e0, e1):
             nc.vector.quantize_mx(
                 out=own_codes[:, s, C * e0 : C * e1].bitcast(FP8X4),
-                scales=own_scales[:, s, C * e0 : C * e1],
+                scales=own_scales[s][:, C * e0 : C * e1],
                 in_=grouped[s][:, C * e0 : C * e1, :, :].rearrange("p c u e -> p (c u e)"),
             )
 
@@ -107,7 +102,7 @@ def tile_moe_loc_lin_gelu_kernel(tc, x_words, x_scales, xo, w_words, w_scales, g
                 lhsT=w_codes[:, PASSES * e + s, :].bitcast(FP4X4),
                 lhsT_scale=w_scale_rows[:, PASSES * e + s, :],
                 rhs=codes[:, s, C * e : C * (e + 1)].bitcast(FP8X4),
-                rhs_scale=scales[:, s, C * e : C * (e + 1)],
+                rhs_scale=scales[s][:, C * e : C * (e + 1)],
                 start=(s == 0),
                 stop=(s == PASSES - 1),
             )
@@ -115,54 +110,62 @@ def tile_moe_loc_lin_gelu_kernel(tc, x_words, x_scales, xo, w_words, w_scales, g
         def load_far_words(s):
             nc.sync.dma_start(out=far_words[s][:], in_=x_words[s].rearrange("p t d -> p (t d)").bitcast(I32))
 
-        def gather_far_words(s):
-            nc.vector.tensor_copy(far_codes[:, s, :], far_words[s][:].bitcast(U32).indirect(far_list[:]))
+        def gather_far_words(s, e0, e1):
+            nc.vector.tensor_copy(
+                far_codes[:, s, C * e0 : C * e1],
+                far_words[s][:].bitcast(U32).indirect(far_list[:, COLS_PER_EXPERT * e0 : COLS_PER_EXPERT * e1]),
+            )
 
-        nc.vector.memset(far_scale_rows[:, 0, :].bitcast(I32), 0)
-        nc.gpsimd.memset(far_scale_rows[:, 1, :].bitcast(I32), 0)
-        nc.gpsimd.memset(warm_in[:], 0.0)
-        nc.gpsimd.memset(w_scale_rows[:].rearrange("p g n -> p (g n)").bitcast(I32), 0)
-        nc.gpsimd.memset(own[:], 0.0)
+        nc.vector.memset(far_scale_rows[:].bitcast(I32), 0)
+        nc.vector.memset(warm_in[:], 0.0)
+        nc.vector.memset(w_scale_rows[:].rearrange("p g n -> p (g n)").bitcast(I32), 0)
+        nc.vector.memset(far_scales[1][:].bitcast(I32), 0)
+        nc.vector.memset(own[:], 0.0)
 
         nc.sync.dma_start(far_list[:], offs2)
         load_far_words(0)
-        gather_far_words(0)
+        gather_far_words(0, 0, E)
         nc.sync.dma_start(own_list[:], offs)
         x_rows = x_scales.rearrange("s (q r) t -> r q s t", r=4)
         for r in range(4):
-            nc.sync.dma_start(out=far_scale_rows[r:P:32, :, :].bitcast(I32), in_=x_rows[r].bitcast(I32))
+            nc.sync.dma_start(out=far_scale_rows[r:P:16, :].bitcast(I32), in_=x_rows[r].bitcast(I32))
         nc.scalar.activation(warm_out[:], warm_in[:], GELU)
-        for s in range(PASSES):
-            nc.vector.tensor_copy(far_scales[:, s, :], far_scale_rows[:, s, :].indirect(far_list[:]))
+        nc.vector.tensor_copy(far_scales[0][:], far_scale_rows[:].indirect(far_list[:]))
 
         load_pair(0)
         gather_pair(0, 0, E)
         load_pair(1)
-        gather_pair(1, 0, E)
-        interleave(0, 0, E)
+        halves = [(0, 2), (2, 4)]
+        for e0, e1 in halves:
+            gather_pair(1, e0, e1)
+        for e0, e1 in halves:
+            interleave(nc.vector.tensor_copy, 0, e0, e1)
         load_pair(2)
-        quantise(0, 0, E)
+        for e0, e1 in halves:
+            quantise(0, e0, e1)
         gather_pair(2, 0, E)
         load_pair(3)
         w_rows = w_scales.rearrange("e s (q r) n -> r q (e s) n", r=4)
         for r in range(4):
             nc.sync.dma_start(out=w_scale_rows[r:P:32, :, :].bitcast(I32), in_=w_rows[r].bitcast(I32))
+
         nc.sync.dma_start(out=w_codes[:].bitcast(I32), in_=w_words.rearrange("e s p b -> p (e s) b").bitcast(I32))
         load_far_words(1)
         nc.sync.dma_start(out=gate_sb[:], in_=gate)
+        nc.sync.dma_start(out=far_scales[1][0 : P - 16, :].bitcast(I32), in_=far_scales[0][16:P, :].bitcast(I32))
 
-        halves = [(0, 2), (2, 4)]
         for e0, e1 in halves:
             gather_pair(3, e0, e1)
+        for (e0, e1), copy in zip(halves, (nc.vector.tensor_copy, nc.scalar.copy)):
+            interleave(copy, 1, e0, e1)
+        for e in range(E):
+            expert_pass(y_banks[e][:], own_codes, own_scales, e, 0)
         for e0, e1 in halves:
-            interleave(1, e0, e1)
-        for h, (e0, e1) in enumerate(halves):
             quantise(1, e0, e1)
             for e in range(e0, e1):
-                for s in range(PASSES):
-                    expert_pass(y_banks[h][:, C * (e - e0) : C * (e - e0 + 1)], own_codes, own_scales, e, s)
-            nc.scalar.activation(y_sb[:, C * e0 : C * e1], y_banks[h][:], GELU)
-        gather_far_words(1)
+                expert_pass(y_banks[e][:], own_codes, own_scales, e, 1)
+                nc.scalar.activation(y_sb[:, C * e : C * (e + 1)], y_banks[e][:], GELU)
+        gather_far_words(1, 0, E)
         for e in range(E):
             for s in range(PASSES):
                 expert_pass(z_bank[:, C * e : C * (e + 1)], far_codes, far_scales, e, s)

@@ -22,10 +22,10 @@ FP4X4 = mybir.dt.float4_e2m1fn_x4
 GELU = mybir.ActivationFunctionType.Gelu_apprx_tanh
 MULT = mybir.AluOpType.mult
 
-LOADS = [[(0, 512), (512, 1024)]] * 4
+LOADS = [[(0, 1024)], [(0, 1024)], [(0, 512), (512, 1024)], [(0, 512), (512, 1024)]]
 CASTS = [
-    [(0, 512, "s"), (512, 768, "s"), (768, 1024, "v")],
-    [(0, 512, "s"), (512, 800, "s"), (800, 1024, "v")],
+    [(0, 448, "s"), (448, 1024, "v")],
+    [(0, 416, "s"), (416, 1024, "v")],
     [(0, 512, "s"), (512, 1024, "s")],
     [(0, 512, "s"), (512, 800, "s"), (800, 1024, "v")],
 ]

@@ -27,7 +27,7 @@ CASTS = [
     [(0, 448, "s"), (448, 1024, "v")],
     [(0, 416, "s"), (416, 1024, "v")],
     [(0, 512, "s"), (512, 1024, "s")],
-    [(0, 512, "s"), (512, 800, "s"), (800, 1024, "v")],
+    [(0, 512, "s"), (512, 736, "s"), (736, 1024, "v")],
 ]
 
 
@@ -37,15 +37,15 @@ def tile_moe_loc_lin_gelu_kernel(tc, x_words, x_scales, xo, w_words, w_scales, g
         keep = ctx.enter_context(tc.tile_pool(name="keep", bufs=1))
         psum = ctx.enter_context(tc.psum_pool(name="psum", bufs=1))
 
-        def sbuf(name, shape, dtype):
-            return keep.tile(shape, dtype, name=name, align_bytes=64)
+        def sbuf(name, shape, dtype, tag=None):
+            return keep.tile(shape, dtype, name=name, tag=tag or name, align_bytes=64)
 
         own_list = keep.tile([P, LIST_COLS], U16, name="own_list")
         far_list = keep.tile([P, LIST_COLS], U16, name="far_list")
         far_scale_rows = sbuf("far_scale_rows", [P, Q], U8)
         w_scale_rows = sbuf("w_scale_rows", [P, E * PASSES, N], U8)
         w_codes = sbuf("w_codes", [P, E * PASSES, 2 * N], U8)
-        far_words = [sbuf(f"far_words{s}", [P, Q], I32) for s in range(PASSES)]
+        far_words = [sbuf("far_words0", [P, Q], I32)]
         far_codes = sbuf("far_codes", [P, PASSES, SLOTS], U32)
         far_scales = [sbuf(f"far_scales{s}", [P, SLOTS], U8) for s in range(PASSES)]
         pairs = [sbuf(f"pairs{i}", [P, T, 2], BF16) for i in range(4)]
@@ -53,7 +53,6 @@ def tile_moe_loc_lin_gelu_kernel(tc, x_words, x_scales, xo, w_words, w_scales, g
         grouped = [sbuf(f"grouped{s}", [P, SLOTS, 2, 2], BF16) for s in range(PASSES)]
         own_codes = sbuf("own_codes", [P, PASSES, SLOTS], U32)
         own_scales = [sbuf(f"own_scales{s}", [P, SLOTS], U8) for s in range(PASSES)]
-        gate_sb = sbuf("gate_sb", [P, SLOTS], F32)
         y_sb = sbuf("y_sb", [P, SLOTS], F32)
         z_sb = sbuf("z_sb", [P, SLOTS], F32)
         own = sbuf("own", [P, T], F32)
@@ -150,13 +149,15 @@ def tile_moe_loc_lin_gelu_kernel(tc, x_words, x_scales, xo, w_words, w_scales, g
             nc.sync.dma_start(out=w_scale_rows[r:P:32, :, :].bitcast(I32), in_=w_rows[r].bitcast(I32))
 
         nc.sync.dma_start(out=w_codes[:].bitcast(I32), in_=w_words.rearrange("e s p b -> p (e s) b").bitcast(I32))
-        load_far_words(1)
-        nc.sync.dma_start(out=gate_sb[:], in_=gate)
         nc.sync.dma_start(out=far_scales[1][0 : P - 16, :].bitcast(I32), in_=far_scales[0][16:P, :].bitcast(I32))
+        far_words.append(sbuf("far_words1", [P, Q], I32, tag="far_scale_rows"))
+        load_far_words(1)
+        gate_sb = sbuf("gate_sb", [P, SLOTS], F32, tag="raw0_0")
+        nc.sync.dma_start(out=gate_sb[:], in_=gate)
 
         for e0, e1 in halves:
             gather_pair(3, e0, e1)
-        for (e0, e1), copy in zip(halves, (nc.vector.tensor_copy, nc.scalar.copy)):
+        for (e0, e1), copy in zip(halves, (nc.vector.tensor_copy, nc.vector.tensor_copy)):
             interleave(copy, 1, e0, e1)
         for e in range(E):
             expert_pass(y_banks[e][:], own_codes, own_scales, e, 0)

@@ -59,7 +59,7 @@ def tile_moe_loc_lin_gelu_kernel(tc, x_words, x_scales, xo, w_words, w_scales, g
         warm_in = sbuf("warm_in", [P, 8], F32)
         warm_out = sbuf("warm_out", [P, 8], F32)
         y_banks = [psum.tile([P, C], F32, name=f"y_bank{e}") for e in range(E)]
-        z_bank = psum.tile([P, SLOTS], F32, name="z_bank")
+        z_banks = [psum.tile([P, C], F32, name=f"z_bank{e}") for e in range(E)]
 
         xo_pairs = xo.rearrange("(s p u e) t -> s u p e t", s=PASSES, p=P, u=2, e=2)
 
@@ -121,8 +121,8 @@ def tile_moe_loc_lin_gelu_kernel(tc, x_words, x_scales, xo, w_words, w_scales, g
         nc.vector.memset(far_scales[1][:].bitcast(I32), 0)
         nc.vector.memset(own[:], 0.0)
 
-        nc.sync.dma_start(far_list[:], offs2)
         load_far_words(0)
+        nc.sync.dma_start(far_list[:], offs2)
         gather_far_words(0, 0, E)
         nc.sync.dma_start(own_list[:], offs)
         x_rows = x_scales.rearrange("s (q r) t -> r q s t", r=4)
@@ -161,16 +161,17 @@ def tile_moe_loc_lin_gelu_kernel(tc, x_words, x_scales, xo, w_words, w_scales, g
             interleave(copy, 1, e0, e1)
         for e in range(E):
             expert_pass(y_banks[e][:], own_codes, own_scales, e, 0)
-        for e0, e1 in halves:
+        for e in range(E):
+            expert_pass(z_banks[e][:], far_codes, far_scales, e, 0)
+        for e0, e1 in [(0, 2), (2, 3), (3, 4)]:
             quantise(1, e0, e1)
             for e in range(e0, e1):
                 expert_pass(y_banks[e][:], own_codes, own_scales, e, 1)
                 nc.scalar.activation(y_sb[:, C * e : C * (e + 1)], y_banks[e][:], GELU)
         gather_far_words(1, 0, E)
         for e in range(E):
-            for s in range(PASSES):
-                expert_pass(z_bank[:, C * e : C * (e + 1)], far_codes, far_scales, e, s)
-        nc.scalar.activation(z_sb[:], z_bank[:], GELU)
+            expert_pass(z_banks[e][:], far_codes, far_scales, e, 1)
+            nc.scalar.activation(z_sb[:, C * e : C * (e + 1)], z_banks[e][:], GELU)
         nc.scalar.dma_start(out=out[:, T:], in_=z_sb[:])
         nc.vector.tensor_tensor(own[:].indirect(own_list[:]), y_sb[:], gate_sb[:], MULT)
         nc.sync.dma_start(out=out[:, :T], in_=own[:])

@@ -44,7 +44,7 @@ def tile_moe_loc_lin_gelu_kernel(tc, x_words, x_scales, xo, w_words, w_scales, g
         far_list = keep.tile([P, LIST_COLS], U16, name="far_list")
         far_scale_rows = sbuf("far_scale_rows", [P, Q], U8)
         w_scale_rows = sbuf("w_scale_rows", [P, E * PASSES, N], U8)
-        w_codes = sbuf("w_codes", [P, E * PASSES, 2 * N], U8)
+        w_codes = [sbuf(f"w_codes{h}", [P, E, 2 * N], U8) for h in range(2)]
         far_words = [sbuf("far_words0", [P, Q], I32)]
         far_codes = sbuf("far_codes", [P, PASSES, SLOTS], U32)
         far_scales = [sbuf(f"far_scales{s}", [P, SLOTS], U8) for s in range(PASSES)]
@@ -98,7 +98,7 @@ def tile_moe_loc_lin_gelu_kernel(tc, x_words, x_scales, xo, w_words, w_scales, g
         def expert_pass(bank, codes, scales, e, s):
             nc.tensor.matmul_mx(
                 out=bank,
-                lhsT=w_codes[:, PASSES * e + s, :].bitcast(FP4X4),
+                lhsT=w_codes[e // 2][:, PASSES * (e % 2) + s, :].bitcast(FP4X4),
                 lhsT_scale=w_scale_rows[:, PASSES * e + s, :],
                 rhs=codes[:, s, C * e : C * (e + 1)].bitcast(FP8X4),
                 rhs_scale=scales[s][:, C * e : C * (e + 1)],
@@ -148,10 +148,12 @@ def tile_moe_loc_lin_gelu_kernel(tc, x_words, x_scales, xo, w_words, w_scales, g
         for r in range(4):
             nc.sync.dma_start(out=w_scale_rows[r:P:32, :, :].bitcast(I32), in_=w_rows[r].bitcast(I32))
 
-        nc.sync.dma_start(out=w_codes[:].bitcast(I32), in_=w_words.rearrange("e s p b -> p (e s) b").bitcast(I32))
-        nc.sync.dma_start(out=far_scales[1][0 : P - 16, :].bitcast(I32), in_=far_scales[0][16:P, :].bitcast(I32))
-        far_words.append(sbuf("far_words1", [P, Q], I32, tag="far_scale_rows"))
+        w_view = w_words.rearrange("e s p b -> p (e s) b").bitcast(I32)
+        nc.sync.dma_start(out=w_codes[0][:].bitcast(I32), in_=w_view[:, 0:E, :])
+        far_words.append(sbuf("far_words1", [P, Q], I32))
         load_far_words(1)
+        nc.sync.dma_start(out=w_codes[1][:].bitcast(I32), in_=w_view[:, E : 2 * E, :])
+        nc.sync.dma_start(out=far_scales[1][0 : P - 16, :].bitcast(I32), in_=far_scales[0][16:P, :].bitcast(I32))
         gate_sb = sbuf("gate_sb", [P, SLOTS], F32, tag="raw0_0")
         nc.sync.dma_start(out=gate_sb[:], in_=gate)
 

@@ -46,12 +46,12 @@ def tile_moe_loc_lin_gelu_kernel(tc, x_words, x_scales, xo, w_words, w_scales, g
         w_scale_rows = sbuf("w_scale_rows", [P, E * PASSES, N], U8)
         w_codes = [sbuf(f"w_codes{h}", [P, E, 2 * N], U8) for h in range(2)]
         far_words = [sbuf("far_words0", [P, Q], I32)]
-        far_codes = sbuf("far_codes", [P, PASSES, SLOTS], U32)
+        far_codes = [sbuf("far_codes0", [P, SLOTS], U32)]
         far_scales = [sbuf(f"far_scales{s}", [P, SLOTS], U8) for s in range(PASSES)]
         pairs = [sbuf(f"pairs{i}", [P, T, 2], BF16) for i in range(4)]
         picked = [sbuf(f"picked{s}", [P, 2, 2 * SLOTS], BF16) for s in range(PASSES)]
-        grouped = [sbuf(f"grouped{s}", [P, SLOTS, 2, 2], BF16) for s in range(PASSES)]
-        own_codes = sbuf("own_codes", [P, PASSES, SLOTS], U32)
+        grouped = [[sbuf(f"grouped{s}_{h}", [P, SLOTS // 2, 2, 2], BF16) for h in range(2)] for s in range(PASSES)]
+        own_codes = [sbuf(f"own_codes{s}", [P, SLOTS], U32) for s in range(PASSES)]
         own_scales = [sbuf(f"own_scales{s}", [P, SLOTS], U8) for s in range(PASSES)]
         y_sb = sbuf("y_sb", [P, SLOTS], F32)
         z_sb = sbuf("z_sb", [P, SLOTS], F32)
@@ -84,23 +84,23 @@ def tile_moe_loc_lin_gelu_kernel(tc, x_words, x_scales, xo, w_words, w_scales, g
 
         def interleave(copy, s, e0, e1):
             copy(
-                grouped[s][:, C * e0 : C * e1, :, :].rearrange("p c u e -> p c (u e)").bitcast(F32),
+                grouped[s][e0 // 2][:].rearrange("p c u e -> p c (u e)").bitcast(F32),
                 picked[s][:, :, 2 * C * e0 : 2 * C * e1].bitcast(F32).rearrange("p u c -> p c u"),
             )
 
         def quantise(s, e0, e1):
             nc.vector.quantize_mx(
-                out=own_codes[:, s, C * e0 : C * e1].bitcast(FP8X4),
+                out=own_codes[s][:, C * e0 : C * e1].bitcast(FP8X4),
                 scales=own_scales[s][:, C * e0 : C * e1],
-                in_=grouped[s][:, C * e0 : C * e1, :, :].rearrange("p c u e -> p (c u e)"),
+                in_=grouped[s][e0 // 2][:, C * (e0 % 2) : C * (e0 % 2 + e1 - e0), :, :].rearrange("p c u e -> p (c u e)"),
             )
 
         def expert_pass(bank, codes, scales, e, s):
             nc.tensor.matmul_mx(
                 out=bank,
-                lhsT=w_codes[e // 2][:, PASSES * (e % 2) + s, :].bitcast(FP4X4),
+                lhsT=w_codes[s][:, e, :].bitcast(FP4X4),
                 lhsT_scale=w_scale_rows[:, PASSES * e + s, :],
-                rhs=codes[:, s, C * e : C * (e + 1)].bitcast(FP8X4),
+                rhs=codes[s][:, C * e : C * (e + 1)].bitcast(FP8X4),
                 rhs_scale=scales[s][:, C * e : C * (e + 1)],
                 start=(s == 0),
                 stop=(s == PASSES - 1),
@@ -111,7 +111,7 @@ def tile_moe_loc_lin_gelu_kernel(tc, x_words, x_scales, xo, w_words, w_scales, g
 
         def gather_far_words(s, e0, e1):
             nc.vector.tensor_copy(
-                far_codes[:, s, C * e0 : C * e1],
+                far_codes[s][:, C * e0 : C * e1],
                 far_words[s][:].bitcast(U32).indirect(far_list[:, COLS_PER_EXPERT * e0 : COLS_PER_EXPERT * e1]),
             )
 
@@ -148,11 +148,11 @@ def tile_moe_loc_lin_gelu_kernel(tc, x_words, x_scales, xo, w_words, w_scales, g
         for r in range(4):
             nc.sync.dma_start(out=w_scale_rows[r:P:32, :, :].bitcast(I32), in_=w_rows[r].bitcast(I32))
 
-        w_view = w_words.rearrange("e s p b -> p (e s) b").bitcast(I32)
-        nc.sync.dma_start(out=w_codes[0][:].bitcast(I32), in_=w_view[:, 0:E, :])
+        w_view = w_words.rearrange("e s p b -> s p e b").bitcast(I32)
+        nc.sync.dma_start(out=w_codes[0][:].bitcast(I32), in_=w_view[0])
         far_words.append(sbuf("far_words1", [P, Q], I32))
         load_far_words(1)
-        nc.sync.dma_start(out=w_codes[1][:].bitcast(I32), in_=w_view[:, E : 2 * E, :])
+        nc.sync.dma_start(out=w_codes[1][:].bitcast(I32), in_=w_view[1])
         nc.sync.dma_start(out=far_scales[1][0 : P - 16, :].bitcast(I32), in_=far_scales[0][16:P, :].bitcast(I32))
         gate_sb = sbuf("gate_sb", [P, SLOTS], F32, tag="raw0_0")
         nc.sync.dma_start(out=gate_sb[:], in_=gate)
@@ -170,6 +170,7 @@ def tile_moe_loc_lin_gelu_kernel(tc, x_words, x_scales, xo, w_words, w_scales, g
             for e in range(e0, e1):
                 expert_pass(y_banks[e][:], own_codes, own_scales, e, 1)
                 nc.scalar.activation(y_sb[:, C * e : C * (e + 1)], y_banks[e][:], GELU)
+        far_codes.append(sbuf("far_codes1", [P, SLOTS], U32, tag="grouped1_0"))
         gather_far_words(1, 0, E)
         for e in range(E):
             expert_pass(z_banks[e][:], far_codes, far_scales, e, 1)

@@ -20,14 +20,14 @@ U8 = mybir.dt.uint8
 FP8X4 = mybir.dt.float8_e4m3fn_x4
 FP4X4 = mybir.dt.float4_e2m1fn_x4
 GELU = mybir.ActivationFunctionType.Gelu_apprx_tanh
+COPY = mybir.ActivationFunctionType.Copy
 MULT = mybir.AluOpType.mult
 
-LOADS = [[(0, 1024)], [(0, 1024)], [(0, 512), (512, 1024)], [(0, 512), (512, 1024)]]
+LOADS = [[(0, 1024)], [(0, 1024)], [(0, 512), (512, 1024)]]
 CASTS = [
     [(0, 448, "s"), (448, 1024, "v")],
     [(0, 416, "s"), (416, 1024, "v")],
     [(0, 512, "s"), (512, 1024, "s")],
-    [(0, 512, "s"), (512, 736, "s"), (736, 1024, "v")],
 ]
 
 
@@ -48,9 +48,12 @@ def tile_moe_loc_lin_gelu_kernel(tc, x_words, x_scales, xo, w_words, w_scales, g
         far_words = [sbuf("far_words0", [P, Q], I32)]
         far_codes = [sbuf("far_codes0", [P, SLOTS], U32)]
         far_scales = [sbuf(f"far_scales{s}", [P, SLOTS], U8) for s in range(PASSES)]
-        pairs = [sbuf(f"pairs{i}", [P, T, 2], BF16) for i in range(4)]
-        picked = [sbuf(f"picked{s}", [P, 2, 2 * SLOTS], BF16) for s in range(PASSES)]
-        grouped = [[sbuf(f"grouped{s}_{h}", [P, SLOTS // 2, 2, 2], BF16) for h in range(2)] for s in range(PASSES)]
+        pairs = [sbuf(f"pairs{i}", [P, T, 2], BF16) for i in range(3)]
+        picked = sbuf("picked", [P, 2, 2 * SLOTS], BF16)
+        grouped = [sbuf(f"grouped0_{h}", [P, SLOTS // 2, 2, 2], BF16) for h in range(2)]
+        woven = [sbuf(f"woven{e}", [P, C, 4], BF16) for e in range(E)]
+        rows = [sbuf(f"row{j}", [P, T], F32) for j in range(2)]
+        planes = [sbuf(f"plane{j}", [P, T], BF16) for j in range(2)]
         own_codes = [sbuf(f"own_codes{s}", [P, SLOTS], U32) for s in range(PASSES)]
         own_scales = [sbuf(f"own_scales{s}", [P, SLOTS], U8) for s in range(PASSES)]
         y_sb = sbuf("y_sb", [P, SLOTS], F32)
@@ -78,22 +81,25 @@ def tile_moe_loc_lin_gelu_kernel(tc, x_words, x_scales, xo, w_words, w_scales, g
         def gather_pair(i, e0, e1):
             window = pairs[i][:].rearrange("p c e -> p (c e)").bitcast(U32)
             nc.vector.tensor_copy(
-                picked[i // 2][:, i % 2, 2 * C * e0 : 2 * C * e1].bitcast(U32),
+                picked[:, i % 2, 2 * C * e0 : 2 * C * e1].bitcast(U32),
                 window.indirect(own_list[:, COLS_PER_EXPERT * e0 : COLS_PER_EXPERT * e1]),
             )
 
         def interleave(copy, s, e0, e1):
             copy(
-                grouped[s][e0 // 2][:].rearrange("p c u e -> p c (u e)").bitcast(F32),
-                picked[s][:, :, 2 * C * e0 : 2 * C * e1].bitcast(F32).rearrange("p u c -> p c u"),
+                grouped[e0 // 2][:].rearrange("p c u e -> p c (u e)").bitcast(F32),
+                picked[:, :, 2 * C * e0 : 2 * C * e1].bitcast(F32).rearrange("p u c -> p c u"),
             )
 
         def quantise(s, e0, e1):
             nc.vector.quantize_mx(
                 out=own_codes[s][:, C * e0 : C * e1].bitcast(FP8X4),
                 scales=own_scales[s][:, C * e0 : C * e1],
-                in_=grouped[s][e0 // 2][:, C * (e0 % 2) : C * (e0 % 2 + e1 - e0), :, :].rearrange("p c u e -> p (c u e)"),
+                in_=grouped[e0 // 2][:].rearrange("p c u e -> p (c u e)") if s == 0 else woven[e0][:].rearrange("p c t -> p (c t)"),
             )
+
+        def offsets(e):
+            return own_list[:, COLS_PER_EXPERT * e : COLS_PER_EXPERT * (e + 1)]
 
         def expert_pass(bank, codes, scales, e, s):
             nc.tensor.matmul_mx(
@@ -142,35 +148,40 @@ def tile_moe_loc_lin_gelu_kernel(tc, x_words, x_scales, xo, w_words, w_scales, g
         load_pair(2)
         for e0, e1 in halves:
             quantise(0, e0, e1)
-        gather_pair(2, 0, E)
-        load_pair(3)
+        window = pairs[2][:].rearrange("p c e -> p (c e)").bitcast(U32)
+        for e in range(E):
+            nc.vector.tensor_copy(woven[e][:].bitcast(U32)[:, :, 0], window.indirect(offsets(e)))
+        for j in range(2):
+            nc.sync.dma_start(out=rows[j][:], in_=xo_pairs[1][1][:, j, :])
+            nc.scalar.copy(planes[j][:], rows[j][:])
         w_rows = w_scales.rearrange("e s (q r) n -> r q (e s) n", r=4)
         for r in range(4):
             nc.sync.dma_start(out=w_scale_rows[r:P:32, :, :].bitcast(I32), in_=w_rows[r].bitcast(I32))
 
         w_view = w_words.rearrange("e s p b -> s p e b").bitcast(I32)
         nc.sync.dma_start(out=w_codes[0][:].bitcast(I32), in_=w_view[0])
+        nc.sync.dma_start(out=w_codes[1][:].bitcast(I32), in_=w_view[1])
         far_words.append(sbuf("far_words1", [P, Q], I32))
         load_far_words(1)
-        nc.sync.dma_start(out=w_codes[1][:].bitcast(I32), in_=w_view[1])
         nc.sync.dma_start(out=far_scales[1][0 : P - 16, :].bitcast(I32), in_=far_scales[0][16:P, :].bitcast(I32))
         gate_sb = sbuf("gate_sb", [P, SLOTS], F32, tag="raw0_0")
         nc.sync.dma_start(out=gate_sb[:], in_=gate)
 
-        for e0, e1 in halves:
-            gather_pair(3, e0, e1)
-        for (e0, e1), copy in zip(halves, (nc.vector.tensor_copy, nc.vector.tensor_copy)):
-            interleave(copy, 1, e0, e1)
+        for j in range(2):
+            for e in range(2):
+                nc.vector.tensor_copy(woven[e][:, :, 2 + j], rows[j][:].indirect(offsets(e)))
+            for e in range(2, E):
+                nc.scalar.activation(woven[e][:, :, 2 + j], planes[j][:].indirect(offsets(e)), COPY)
         for e in range(E):
             expert_pass(y_banks[e][:], own_codes, own_scales, e, 0)
         for e in range(E):
             expert_pass(z_banks[e][:], far_codes, far_scales, e, 0)
-        for e0, e1 in [(0, 2), (2, 3), (3, 4)]:
+        for e0, e1 in [(0, 1), (1, 2), (2, 3), (3, 4)]:
             quantise(1, e0, e1)
             for e in range(e0, e1):
                 expert_pass(y_banks[e][:], own_codes, own_scales, e, 1)
                 nc.scalar.activation(y_sb[:, C * e : C * (e + 1)], y_banks[e][:], GELU)
-        far_codes.append(sbuf("far_codes1", [P, SLOTS], U32, tag="grouped1_0"))
+        far_codes.append(sbuf("far_codes1", [P, SLOTS], U32, tag="woven1"))
         gather_far_words(1, 0, E)
         for e in range(E):
             expert_pass(z_banks[e][:], far_codes, far_scales, e, 1)

@@ -22,6 +22,11 @@ FP4X4 = mybir.dt.float4_e2m1fn_x4
 GELU = mybir.ActivationFunctionType.Gelu_apprx_tanh
 COPY = mybir.ActivationFunctionType.Copy
 MULT = mybir.AluOpType.mult
+ADD = mybir.AluOpType.add
+SPLIT = 192
+ROUND_SPLIT = [512, 768]
+SCALAR_PIECES = [(192, 384), (384, 512)]
+PAIR_PIECES = [(192, 384), (384, 512), (0, 192)]
 
 LOADS = [[(0, 1024)], [(0, 1024)], [(0, 512), (512, 1024)]]
 CASTS = [
@@ -51,7 +56,7 @@ def tile_moe_loc_lin_gelu_kernel(tc, x_words, x_scales, xo, w_words, w_scales, g
         pairs = [sbuf(f"pairs{i}", [P, T, 2], BF16) for i in range(3)]
         picked = sbuf("picked", [P, 2, 2 * SLOTS], BF16)
         grouped = [sbuf(f"grouped0_{h}", [P, SLOTS // 2, 2, 2], BF16) for h in range(2)]
-        woven = [sbuf(f"woven{e}", [P, C, 4], BF16) for e in range(E)]
+        woven = sbuf("woven", [P, SLOTS, 4], BF16)
         rows = [sbuf(f"row{j}", [P, T], F32) for j in range(2)]
         planes = [sbuf(f"plane{j}", [P, T], BF16) for j in range(2)]
         own_codes = [sbuf(f"own_codes{s}", [P, SLOTS], U32) for s in range(PASSES)]
@@ -95,11 +100,11 @@ def tile_moe_loc_lin_gelu_kernel(tc, x_words, x_scales, xo, w_words, w_scales, g
             nc.vector.quantize_mx(
                 out=own_codes[s][:, C * e0 : C * e1].bitcast(FP8X4),
                 scales=own_scales[s][:, C * e0 : C * e1],
-                in_=grouped[e0 // 2][:].rearrange("p c u e -> p (c u e)") if s == 0 else woven[e0][:].rearrange("p c t -> p (c t)"),
+                in_=grouped[e0 // 2][:].rearrange("p c u e -> p (c u e)") if s == 0 else woven[:, C * e0 : C * e1, :].rearrange("p c t -> p (c t)"),
             )
 
-        def offsets(e):
-            return own_list[:, COLS_PER_EXPERT * e : COLS_PER_EXPERT * (e + 1)]
+        def offsets(a, b):
+            return own_list[:, a // 16 : b // 16]
 
         def expert_pass(bank, codes, scales, e, s):
             nc.tensor.matmul_mx(
@@ -149,11 +154,14 @@ def tile_moe_loc_lin_gelu_kernel(tc, x_words, x_scales, xo, w_words, w_scales, g
         for e0, e1 in halves:
             quantise(0, e0, e1)
         window = pairs[2][:].rearrange("p c e -> p (c e)").bitcast(U32)
-        for e in range(E):
-            nc.vector.tensor_copy(woven[e][:].bitcast(U32)[:, :, 0], window.indirect(offsets(e)))
+        for a, b in PAIR_PIECES:
+            nc.vector.tensor_copy(woven[:].bitcast(U32)[:, a:b, 0], window.indirect(offsets(a, b)))
         for j in range(2):
             nc.sync.dma_start(out=rows[j][:], in_=xo_pairs[1][1][:, j, :])
-            nc.scalar.copy(planes[j][:], rows[j][:])
+            cut = ROUND_SPLIT[j]
+            nc.gpsimd.tensor_scalar(planes[j][:, :cut], rows[j][:, :cut], 1.0, 0.0, MULT, ADD)
+            if j == 0:
+                nc.scalar.copy(planes[j][:, cut:], rows[j][:, cut:])
         w_rows = w_scales.rearrange("e s (q r) n -> r q (e s) n", r=4)
         for r in range(4):
             nc.sync.dma_start(out=w_scale_rows[r:P:32, :, :].bitcast(I32), in_=w_rows[r].bitcast(I32))
@@ -168,20 +176,21 @@ def tile_moe_loc_lin_gelu_kernel(tc, x_words, x_scales, xo, w_words, w_scales, g
         nc.sync.dma_start(out=gate_sb[:], in_=gate)
 
         for j in range(2):
-            for e in range(2):
-                nc.vector.tensor_copy(woven[e][:, :, 2 + j], rows[j][:].indirect(offsets(e)))
-            for e in range(2, E):
-                nc.scalar.activation(woven[e][:, :, 2 + j], planes[j][:].indirect(offsets(e)), COPY)
+            nc.vector.tensor_copy(woven[:, :SPLIT, 2 + j], rows[j][:].indirect(offsets(0, SPLIT)))
+            if j == 1 and ROUND_SPLIT[1] < T:
+                nc.scalar.copy(planes[j][:, ROUND_SPLIT[1] :], rows[j][:, ROUND_SPLIT[1] :])
+            for a, b in SCALAR_PIECES:
+                nc.scalar.activation(woven[:, a:b, 2 + j], planes[j][:].indirect(offsets(a, b)), COPY)
         for e in range(E):
             expert_pass(y_banks[e][:], own_codes, own_scales, e, 0)
         for e in range(E):
             expert_pass(z_banks[e][:], far_codes, far_scales, e, 0)
-        for e0, e1 in [(0, 1), (1, 2), (2, 3), (3, 4)]:
+        for e0, e1 in [(0, 2), (2, 3), (3, 4)]:
             quantise(1, e0, e1)
             for e in range(e0, e1):
                 expert_pass(y_banks[e][:], own_codes, own_scales, e, 1)
                 nc.scalar.activation(y_sb[:, C * e : C * (e + 1)], y_banks[e][:], GELU)
-        far_codes.append(sbuf("far_codes1", [P, SLOTS], U32, tag="woven1"))
+        far_codes.append(sbuf("far_codes1", [P, SLOTS], U32, tag="woven"))
         gather_far_words(1, 0, E)
         for e in range(E):
             expert_pass(z_banks[e][:], far_codes, far_scales, e, 1)

@@ -49,7 +49,8 @@ def tile_moe_loc_lin_gelu_kernel(tc, x_words, x_scales, xo, w_words, w_scales, g
         far_list = keep.tile([P, LIST_COLS], U16, name="far_list")
         far_scale_rows = sbuf("far_scale_rows", [P, Q], U8)
         w_scale_rows = sbuf("w_scale_rows", [P, E * PASSES, N], U8)
-        w_codes = [sbuf(f"w_codes{h}", [P, E, 2 * N], U8) for h in range(2)]
+        w_early = sbuf("w_early", [P, (E - 1) * PASSES, 2 * N], U8)
+        w_late = sbuf("w_late", [P, PASSES, 2 * N], U8)
         far_words = [sbuf("far_words0", [P, Q], I32)]
         far_codes = [sbuf("far_codes0", [P, SLOTS], U32)]
         far_scales = [sbuf(f"far_scales{s}", [P, SLOTS], U8) for s in range(PASSES)]
@@ -67,7 +68,6 @@ def tile_moe_loc_lin_gelu_kernel(tc, x_words, x_scales, xo, w_words, w_scales, g
         warm_in = sbuf("warm_in", [P, 8], F32)
         warm_out = sbuf("warm_out", [P, 8], F32)
         y_banks = [psum.tile([P, C], F32, name=f"y_bank{e}") for e in range(E)]
-        z_banks = [psum.tile([P, C], F32, name=f"z_bank{e}") for e in range(E)]
 
         xo_pairs = xo.rearrange("(s p u e) t -> s u p e t", s=PASSES, p=P, u=2, e=2)
 
@@ -109,7 +109,7 @@ def tile_moe_loc_lin_gelu_kernel(tc, x_words, x_scales, xo, w_words, w_scales, g
         def expert_pass(bank, codes, scales, e, s):
             nc.tensor.matmul_mx(
                 out=bank,
-                lhsT=w_codes[s][:, e, :].bitcast(FP4X4),
+                lhsT=(w_early[:, PASSES * e + s, :] if e < E - 1 else w_late[:, s, :]).bitcast(FP4X4),
                 lhsT_scale=w_scale_rows[:, PASSES * e + s, :],
                 rhs=codes[s][:, C * e : C * (e + 1)].bitcast(FP8X4),
                 rhs_scale=scales[s][:, C * e : C * (e + 1)],
@@ -166,14 +166,14 @@ def tile_moe_loc_lin_gelu_kernel(tc, x_words, x_scales, xo, w_words, w_scales, g
         for r in range(4):
             nc.sync.dma_start(out=w_scale_rows[r:P:32, :, :].bitcast(I32), in_=w_rows[r].bitcast(I32))
 
-        w_view = w_words.rearrange("e s p b -> s p e b").bitcast(I32)
-        nc.sync.dma_start(out=w_codes[0][:].bitcast(I32), in_=w_view[0])
-        nc.sync.dma_start(out=w_codes[1][:].bitcast(I32), in_=w_view[1])
+        w_view = w_words.rearrange("e s p b -> p (e s) b").bitcast(I32)
+        nc.sync.dma_start(out=w_early[:].bitcast(I32), in_=w_view[:, : (E - 1) * PASSES, :])
         far_words.append(sbuf("far_words1", [P, Q], I32))
         load_far_words(1)
-        nc.sync.dma_start(out=far_scales[1][0 : P - 16, :].bitcast(I32), in_=far_scales[0][16:P, :].bitcast(I32))
-        gate_sb = sbuf("gate_sb", [P, SLOTS], F32, tag="raw0_0")
+        nc.sync.dma_start(out=w_late[:].bitcast(I32), in_=w_view[:, (E - 1) * PASSES :, :])
+        gate_sb = sbuf("gate_sb", [P, SLOTS], F32)
         nc.sync.dma_start(out=gate_sb[:], in_=gate)
+        nc.sync.dma_start(out=far_scales[1][0 : P - 16, :].bitcast(I32), in_=far_scales[0][16:P, :].bitcast(I32))
 
         for j in range(2):
             nc.vector.tensor_copy(woven[:, :SPLIT, 2 + j], rows[j][:].indirect(offsets(0, SPLIT)))
@@ -181,20 +181,22 @@ def tile_moe_loc_lin_gelu_kernel(tc, x_words, x_scales, xo, w_words, w_scales, g
                 nc.scalar.copy(planes[j][:, ROUND_SPLIT[1] :], rows[j][:, ROUND_SPLIT[1] :])
             for a, b in SCALAR_PIECES:
                 nc.scalar.activation(woven[:, a:b, 2 + j], planes[j][:].indirect(offsets(a, b)), COPY)
-        for e in range(E):
+        for e in range(E - 1):
             expert_pass(y_banks[e][:], own_codes, own_scales, e, 0)
-        for e in range(E):
-            expert_pass(z_banks[e][:], far_codes, far_scales, e, 0)
         for e0, e1 in [(0, 2), (2, 3), (3, 4)]:
             quantise(1, e0, e1)
             for e in range(e0, e1):
+                if e == E - 1:
+                    expert_pass(y_banks[e][:], own_codes, own_scales, e, 0)
                 expert_pass(y_banks[e][:], own_codes, own_scales, e, 1)
                 nc.scalar.activation(y_sb[:, C * e : C * (e + 1)], y_banks[e][:], GELU)
         far_codes.append(sbuf("far_codes1", [P, SLOTS], U32, tag="woven"))
         gather_far_words(1, 0, E)
+        z_bank = psum.tile([P, SLOTS], F32, name="z_bank", tag=f"y_bank{E - 1}")
         for e in range(E):
-            expert_pass(z_banks[e][:], far_codes, far_scales, e, 1)
-            nc.scalar.activation(z_sb[:, C * e : C * (e + 1)], z_banks[e][:], GELU)
+            for s in range(PASSES):
+                expert_pass(z_bank[:, C * e : C * (e + 1)], far_codes, far_scales, e, s)
+        nc.scalar.activation(z_sb[:], z_bank[:], GELU)
         nc.scalar.dma_start(out=out[:, T:], in_=z_sb[:])
         nc.vector.tensor_tensor(own[:].indirect(own_list[:]), y_sb[:], gate_sb[:], MULT)
         nc.sync.dma_start(out=out[:, :T], in_=own[:])

@@ -23,10 +23,11 @@ GELU = mybir.ActivationFunctionType.Gelu_apprx_tanh
 COPY = mybir.ActivationFunctionType.Copy
 MULT = mybir.AluOpType.mult
 ADD = mybir.AluOpType.add
-SPLIT = 192
-ROUND_SPLIT = [512, 768]
-SCALAR_PIECES = [(192, 384), (384, 512)]
-PAIR_PIECES = [(192, 384), (384, 512), (0, 192)]
+SPLIT = 160
+ROUND_SPLIT = 384
+LAST_CUT = 512
+SCALAR_PIECES = [[(160, 512)], [(160, 384), (384, 512)]]
+PAIR_PIECES = [(160, 512), (0, 160)]
 
 LOADS = [[(0, 1024)], [(0, 1024)], [(0, 512), (512, 1024)]]
 CASTS = [
@@ -157,11 +158,14 @@ def tile_moe_loc_lin_gelu_kernel(tc, x_words, x_scales, xo, w_words, w_scales, g
         for a, b in PAIR_PIECES:
             nc.vector.tensor_copy(woven[:].bitcast(U32)[:, a:b, 0], window.indirect(offsets(a, b)))
         for j in range(2):
-            nc.sync.dma_start(out=rows[j][:], in_=xo_pairs[1][1][:, j, :])
-            cut = ROUND_SPLIT[j]
-            nc.gpsimd.tensor_scalar(planes[j][:, :cut], rows[j][:, :cut], 1.0, 0.0, MULT, ADD)
             if j == 0:
-                nc.scalar.copy(planes[j][:, cut:], rows[j][:, cut:])
+                nc.sync.dma_start(out=rows[j][:], in_=xo_pairs[1][1][:, j, :])
+                nc.gpsimd.tensor_scalar(planes[j][:, :ROUND_SPLIT], rows[j][:, :ROUND_SPLIT], 1.0, 0.0, MULT, ADD)
+                nc.scalar.copy(planes[j][:, ROUND_SPLIT:], rows[j][:, ROUND_SPLIT:])
+            else:
+                for c0, c1 in [(0, LAST_CUT), (LAST_CUT, T)]:
+                    nc.sync.dma_start(out=rows[j][:, c0:c1], in_=xo_pairs[1][1][:, j, c0:c1])
+                    nc.gpsimd.tensor_scalar(planes[j][:, c0:c1], rows[j][:, c0:c1], 1.0, 0.0, MULT, ADD)
         w_rows = w_scales.rearrange("e s (q r) n -> r q (e s) n", r=4)
         for r in range(4):
             nc.sync.dma_start(out=w_scale_rows[r:P:32, :, :].bitcast(I32), in_=w_rows[r].bitcast(I32))
@@ -177,9 +181,7 @@ def tile_moe_loc_lin_gelu_kernel(tc, x_words, x_scales, xo, w_words, w_scales, g
 
         for j in range(2):
             nc.vector.tensor_copy(woven[:, :SPLIT, 2 + j], rows[j][:].indirect(offsets(0, SPLIT)))
-            if j == 1 and ROUND_SPLIT[1] < T:
-                nc.scalar.copy(planes[j][:, ROUND_SPLIT[1] :], rows[j][:, ROUND_SPLIT[1] :])
-            for a, b in SCALAR_PIECES:
+            for a, b in SCALAR_PIECES[j]:
                 nc.scalar.activation(woven[:, a:b, 2 + j], planes[j][:].indirect(offsets(a, b)), COPY)
         for e in range(E - 1):
             expert_pass(y_banks[e][:], own_codes, own_scales, e, 0)

@@ -23,11 +23,11 @@ GELU = mybir.ActivationFunctionType.Gelu_apprx_tanh
 COPY = mybir.ActivationFunctionType.Copy
 MULT = mybir.AluOpType.mult
 ADD = mybir.AluOpType.add
-SPLIT = 160
-ROUND_SPLIT = 384
+SPLIT = 192
+ROUND_SPLIT = 320
 LAST_CUT = 512
-SCALAR_PIECES = [[(160, 512)], [(160, 384), (384, 512)]]
-PAIR_PIECES = [(160, 512), (0, 160)]
+SCALAR_PIECES = [[(192, 512)], [(192, 384), (384, 512)]]
+PAIR_PIECES = [(192, 512), (0, 192)]
 
 LOADS = [[(0, 1024)], [(0, 1024)], [(0, 512), (512, 1024)]]
 CASTS = [
@@ -50,8 +50,7 @@ def tile_moe_loc_lin_gelu_kernel(tc, x_words, x_scales, xo, w_words, w_scales, g
         far_list = keep.tile([P, LIST_COLS], U16, name="far_list")
         far_scale_rows = sbuf("far_scale_rows", [P, Q], U8)
         w_scale_rows = sbuf("w_scale_rows", [P, E * PASSES, N], U8)
-        w_early = sbuf("w_early", [P, (E - 1) * PASSES, 2 * N], U8)
-        w_late = sbuf("w_late", [P, PASSES, 2 * N], U8)
+        w_codes = sbuf("w_codes", [P, E * PASSES, 2 * N], U8)
         far_words = [sbuf("far_words0", [P, Q], I32)]
         far_codes = [sbuf("far_codes0", [P, SLOTS], U32)]
         far_scales = [sbuf(f"far_scales{s}", [P, SLOTS], U8) for s in range(PASSES)]
@@ -110,7 +109,7 @@ def tile_moe_loc_lin_gelu_kernel(tc, x_words, x_scales, xo, w_words, w_scales, g
         def expert_pass(bank, codes, scales, e, s):
             nc.tensor.matmul_mx(
                 out=bank,
-                lhsT=(w_early[:, PASSES * e + s, :] if e < E - 1 else w_late[:, s, :]).bitcast(FP4X4),
+                lhsT=w_codes[:, PASSES * e + s, :].bitcast(FP4X4),
                 lhsT_scale=w_scale_rows[:, PASSES * e + s, :],
                 rhs=codes[s][:, C * e : C * (e + 1)].bitcast(FP8X4),
                 rhs_scale=scales[s][:, C * e : C * (e + 1)],
@@ -171,10 +170,9 @@ def tile_moe_loc_lin_gelu_kernel(tc, x_words, x_scales, xo, w_words, w_scales, g
             nc.sync.dma_start(out=w_scale_rows[r:P:32, :, :].bitcast(I32), in_=w_rows[r].bitcast(I32))
 
         w_view = w_words.rearrange("e s p b -> p (e s) b").bitcast(I32)
-        nc.sync.dma_start(out=w_early[:].bitcast(I32), in_=w_view[:, : (E - 1) * PASSES, :])
+        nc.sync.dma_start(out=w_codes[:].bitcast(I32), in_=w_view)
         far_words.append(sbuf("far_words1", [P, Q], I32))
         load_far_words(1)
-        nc.sync.dma_start(out=w_late[:].bitcast(I32), in_=w_view[:, (E - 1) * PASSES :, :])
         gate_sb = sbuf("gate_sb", [P, SLOTS], F32)
         nc.sync.dma_start(out=gate_sb[:], in_=gate)
         nc.sync.dma_start(out=far_scales[1][0 : P - 16, :].bitcast(I32), in_=far_scales[0][16:P, :].bitcast(I32))
@@ -183,13 +181,11 @@ def tile_moe_loc_lin_gelu_kernel(tc, x_words, x_scales, xo, w_words, w_scales, g
             nc.vector.tensor_copy(woven[:, :SPLIT, 2 + j], rows[j][:].indirect(offsets(0, SPLIT)))
             for a, b in SCALAR_PIECES[j]:
                 nc.scalar.activation(woven[:, a:b, 2 + j], planes[j][:].indirect(offsets(a, b)), COPY)
-        for e in range(E - 1):
+        for e in range(E):
             expert_pass(y_banks[e][:], own_codes, own_scales, e, 0)
-        for e0, e1 in [(0, 2), (2, 3), (3, 4)]:
+        for e0, e1 in [(0, 1), (1, 3), (3, 4)]:
             quantise(1, e0, e1)
             for e in range(e0, e1):
-                if e == E - 1:
-                    expert_pass(y_banks[e][:], own_codes, own_scales, e, 0)
                 expert_pass(y_banks[e][:], own_codes, own_scales, e, 1)
                 nc.scalar.activation(y_sb[:, C * e : C * (e + 1)], y_banks[e][:], GELU)
         far_codes.append(sbuf("far_codes1", [P, SLOTS], U32, tag="woven"))

@@ -27,7 +27,7 @@ SPLIT = 192
 ROUND_SPLIT = 320
 LAST_CUT = 512
 SCALAR_PIECES = [[(192, 512)], [(192, 384), (384, 512)]]
-PAIR_PIECES = [(192, 512), (0, 192)]
+EARLY = 352
 
 LOADS = [[(0, 1024)], [(0, 1024)], [(0, 512), (512, 1024)]]
 CASTS = [
@@ -54,11 +54,13 @@ def tile_moe_loc_lin_gelu_kernel(tc, x_words, x_scales, xo, w_words, w_scales, g
         far_words = [sbuf("far_words0", [P, Q], I32)]
         far_codes = [sbuf("far_codes0", [P, SLOTS], U32)]
         far_scales = [sbuf(f"far_scales{s}", [P, SLOTS], U8) for s in range(PASSES)]
-        pairs = [sbuf(f"pairs{i}", [P, T, 2], BF16) for i in range(3)]
+        pair2_and_last_row = sbuf("pair2_and_last_row", [P, 2 * T], F32)
+        pairs = [sbuf(f"pairs{i}", [P, T, 2], BF16) for i in range(2)]
+        pairs.append(pair2_and_last_row[:, :T].bitcast(BF16).rearrange("p (c e) -> p c e", e=2))
         picked = sbuf("picked", [P, 2, 2 * SLOTS], BF16)
         grouped = [sbuf(f"grouped0_{h}", [P, SLOTS // 2, 2, 2], BF16) for h in range(2)]
         woven = sbuf("woven", [P, SLOTS, 4], BF16)
-        rows = [sbuf(f"row{j}", [P, T], F32) for j in range(2)]
+        rows = [sbuf("row0", [P, T], F32), pair2_and_last_row[:, T:]]
         planes = [sbuf(f"plane{j}", [P, T], BF16) for j in range(2)]
         own_codes = [sbuf(f"own_codes{s}", [P, SLOTS], U32) for s in range(PASSES)]
         own_scales = [sbuf(f"own_scales{s}", [P, SLOTS], U8) for s in range(PASSES)]
@@ -153,16 +155,15 @@ def tile_moe_loc_lin_gelu_kernel(tc, x_words, x_scales, xo, w_words, w_scales, g
         load_pair(2)
         for e0, e1 in halves:
             quantise(0, e0, e1)
-        window = pairs[2][:].rearrange("p c e -> p (c e)").bitcast(U32)
-        for a, b in PAIR_PIECES:
-            nc.vector.tensor_copy(woven[:].bitcast(U32)[:, a:b, 0], window.indirect(offsets(a, b)))
+        words = pair2_and_last_row[:].bitcast(U32)
+        nc.vector.tensor_copy(woven[:].bitcast(U32)[:, :EARLY, 0], words[:, :T].indirect(offsets(0, EARLY)))
         for j in range(2):
             if j == 0:
                 nc.sync.dma_start(out=rows[j][:], in_=xo_pairs[1][1][:, j, :])
                 nc.gpsimd.tensor_scalar(planes[j][:, :ROUND_SPLIT], rows[j][:, :ROUND_SPLIT], 1.0, 0.0, MULT, ADD)
                 nc.scalar.copy(planes[j][:, ROUND_SPLIT:], rows[j][:, ROUND_SPLIT:])
             else:
-                for c0, c1 in [(0, LAST_CUT), (LAST_CUT, T)]:
+                for c0, c1 in [(LAST_CUT, T), (0, LAST_CUT)]:
                     nc.sync.dma_start(out=rows[j][:, c0:c1], in_=xo_pairs[1][1][:, j, c0:c1])
                     nc.gpsimd.tensor_scalar(planes[j][:, c0:c1], rows[j][:, c0:c1], 1.0, 0.0, MULT, ADD)
         w_rows = w_scales.rearrange("e s (q r) n -> r q (e s) n", r=4)
@@ -178,9 +179,10 @@ def tile_moe_loc_lin_gelu_kernel(tc, x_words, x_scales, xo, w_words, w_scales, g
         nc.sync.dma_start(out=far_scales[1][0 : P - 16, :].bitcast(I32), in_=far_scales[0][16:P, :].bitcast(I32))
 
         for j in range(2):
-            nc.vector.tensor_copy(woven[:, :SPLIT, 2 + j], rows[j][:].indirect(offsets(0, SPLIT)))
+            nc.vector.tensor_copy(woven[:, :SPLIT, 2 + j], rows[j][:, :].indirect(offsets(0, SPLIT)))
             for a, b in SCALAR_PIECES[j]:
                 nc.scalar.activation(woven[:, a:b, 2 + j], planes[j][:].indirect(offsets(a, b)), COPY)
+        nc.vector.tensor_copy(woven[:].bitcast(U32)[:, EARLY:, 0], words[:, : T + 16].indirect(offsets(EARLY, SLOTS)))
         for e in range(E):
             expert_pass(y_banks[e][:], own_codes, own_scales, e, 0)
         for e0, e1 in [(0, 1), (1, 3), (3, 4)]:

@@ -7,7 +7,6 @@ P = 128
 PASSES = 2
 SLOTS = E * C
 LIST_COLS = SLOTS // 16
-COLS_PER_EXPERT = C // 16
 
 FLOPS = 2 * K * N * 2 * SLOTS
 
@@ -22,19 +21,6 @@ FP4X4 = mybir.dt.float4_e2m1fn_x4
 GELU = mybir.ActivationFunctionType.Gelu_apprx_tanh
 COPY = mybir.ActivationFunctionType.Copy
 MULT = mybir.AluOpType.mult
-ADD = mybir.AluOpType.add
-SPLIT = 192
-ROUND_SPLIT = 320
-LAST_CUT = 512
-SCALAR_PIECES = [[(192, 512)], [(192, 384), (384, 512)]]
-EARLY = 352
-
-LOADS = [[(0, 1024)], [(0, 1024)], [(0, 512), (512, 1024)]]
-CASTS = [
-    [(0, 448, "s"), (448, 1024, "v")],
-    [(0, 416, "s"), (416, 1024, "v")],
-    [(0, 512, "s"), (512, 1024, "s")],
-]
 
 
 def tile_moe_loc_lin_gelu_kernel(tc, x_words, x_scales, xo, w_words, w_scales, gate, offs, offs2, out):
@@ -50,153 +36,162 @@ def tile_moe_loc_lin_gelu_kernel(tc, x_words, x_scales, xo, w_words, w_scales, g
         far_list = keep.tile([P, LIST_COLS], U16, name="far_list")
         far_scale_rows = sbuf("far_scale_rows", [P, Q], U8)
         w_scale_rows = sbuf("w_scale_rows", [P, E * PASSES, N], U8)
-        w_codes = sbuf("w_codes", [P, E * PASSES, 2 * N], U8)
-        far_words = [sbuf("far_words0", [P, Q], I32)]
-        far_codes = [sbuf("far_codes0", [P, SLOTS], U32)]
+        w_codes = [sbuf("w_first", [P, PASSES, 2 * N], U8), sbuf("w_rest", [P, (E - 1) * PASSES, 2 * N], U8)]
+        far_words = [sbuf(f"far_words{s}", [P, Q], I32) for s in range(PASSES)]
         far_scales = [sbuf(f"far_scales{s}", [P, SLOTS], U8) for s in range(PASSES)]
-        pair2_and_last_row = sbuf("pair2_and_last_row", [P, 2 * T], F32)
-        pairs = [sbuf(f"pairs{i}", [P, T, 2], BF16) for i in range(2)]
-        pairs.append(pair2_and_last_row[:, :T].bitcast(BF16).rearrange("p (c e) -> p c e", e=2))
-        picked = sbuf("picked", [P, 2, 2 * SLOTS], BF16)
-        grouped = [sbuf(f"grouped0_{h}", [P, SLOTS // 2, 2, 2], BF16) for h in range(2)]
-        woven = sbuf("woven", [P, SLOTS, 4], BF16)
-        rows = [sbuf("row0", [P, T], F32), pair2_and_last_row[:, T:]]
-        planes = [sbuf(f"plane{j}", [P, T], BF16) for j in range(2)]
+        rows = [sbuf(f"row{j}", [P, T], F32) for j in range(8)]
+        picked = [sbuf(f"picked{s}", [P, 4, SLOTS], BF16) for s in range(PASSES)]
+        woven = [sbuf(f"woven{s}", [P, SLOTS, 4], BF16) for s in range(PASSES)]
         own_codes = [sbuf(f"own_codes{s}", [P, SLOTS], U32) for s in range(PASSES)]
         own_scales = [sbuf(f"own_scales{s}", [P, SLOTS], U8) for s in range(PASSES)]
-        y_sb = sbuf("y_sb", [P, SLOTS], F32)
+        y_sb = [sbuf(f"y{e}", [P, C], F32) for e in range(2)]
+        gated = [sbuf(f"gated{e}", [P, C], F32) for e in range(2)]
         z_sb = sbuf("z_sb", [P, SLOTS], F32)
+        gates = [sbuf(f"gate{h}", [P, 2 * C], F32) for h in range(2)]
         own = sbuf("own", [P, T], F32)
         warm_in = sbuf("warm_in", [P, 8], F32)
         warm_out = sbuf("warm_out", [P, 8], F32)
-        y_banks = [psum.tile([P, C], F32, name=f"y_bank{e}") for e in range(E)]
+        y_banks = [psum.tile([P, C], F32, name="y_bank0"), psum.tile([P, C], F32, name="y_bank1"), psum.tile([P, 2 * C], F32, name="y_bank23")]
+        z_banks = [psum.tile([P, 2 * C], F32, name=f"z_bank{h}") for h in range(2)]
 
-        xo_pairs = xo.rearrange("(s p u e) t -> s u p e t", s=PASSES, p=P, u=2, e=2)
+        xo_rows = xo.rearrange("(s p t) c -> s t p c", s=PASSES, p=P, t=4)
 
-        def load_pair(i):
-            for c0, c1 in LOADS[i]:
-                raw = sbuf(f"raw{i}_{c0}", [P, 2, c1 - c0], F32)
-                nc.sync.dma_start(out=raw[:], in_=xo_pairs[i // 2][i % 2][:, :, c0:c1])
-                for d0, d1, eng in CASTS[i]:
-                    if c0 <= d0 < c1:
-                        src = raw[:, :, d0 - c0 : d1 - c0].rearrange("p e c -> p c e")
-                        if eng == "s":
-                            nc.scalar.copy(pairs[i][:, d0:d1, :], src)
-                        else:
-                            nc.vector.tensor_copy(pairs[i][:, d0:d1, :], src)
-
-        def gather_pair(i, e0, e1):
-            window = pairs[i][:].rearrange("p c e -> p (c e)").bitcast(U32)
-            nc.vector.tensor_copy(
-                picked[:, i % 2, 2 * C * e0 : 2 * C * e1].bitcast(U32),
-                window.indirect(own_list[:, COLS_PER_EXPERT * e0 : COLS_PER_EXPERT * e1]),
-            )
-
-        def interleave(copy, s, e0, e1):
-            copy(
-                grouped[e0 // 2][:].rearrange("p c u e -> p c (u e)").bitcast(F32),
-                picked[:, :, 2 * C * e0 : 2 * C * e1].bitcast(F32).rearrange("p u c -> p c u"),
-            )
-
-        def quantise(s, e0, e1):
-            nc.vector.quantize_mx(
-                out=own_codes[s][:, C * e0 : C * e1].bitcast(FP8X4),
-                scales=own_scales[s][:, C * e0 : C * e1],
-                in_=grouped[e0 // 2][:].rearrange("p c u e -> p (c u e)") if s == 0 else woven[:, C * e0 : C * e1, :].rearrange("p c t -> p (c t)"),
-            )
-
-        def offsets(a, b):
+        def own_offsets(a, b):
             return own_list[:, a // 16 : b // 16]
 
-        def expert_pass(bank, codes, scales, e, s):
+        def far_offsets(a, b):
+            return far_list[:, a // 16 : b // 16]
+
+        def load_row(j):
+            nc.sync.dma_start(out=rows[j][:], in_=xo_rows[j // 4][j % 4])
+
+        def scalar_pick(j, a, b):
+            nc.scalar.activation(picked[j // 4][:, j % 4, a:b], rows[j][:].indirect(own_offsets(a, b)), COPY)
+
+        def vector_pick(j, a, b):
+            nc.vector.tensor_copy(picked[j // 4][:, j % 4, a:b], rows[j][:].indirect(own_offsets(a, b)))
+
+        def vector_pick_woven(j, a, b):
+            nc.vector.tensor_copy(woven[j // 4][:, a:b, j % 4], rows[j][:].indirect(own_offsets(a, b)))
+
+        def weave(s, a, b, count=4):
+            nc.vector.tensor_copy(woven[s][:, a:b, :count], picked[s][:, :count, a:b].rearrange("p t c -> p c t"))
+
+        def quantise(s, a, b):
+            nc.vector.quantize_mx(
+                out=own_codes[s][:, a:b].bitcast(FP8X4),
+                scales=own_scales[s][:, a:b],
+                in_=woven[s][:, a:b, :].rearrange("p c t -> p (c t)"),
+            )
+
+        def expert_pass(bank, codes, scales, e, s, start, stop):
             nc.tensor.matmul_mx(
                 out=bank,
-                lhsT=w_codes[:, PASSES * e + s, :].bitcast(FP4X4),
+                lhsT=(w_codes[0][:, s, :] if e == 0 else w_codes[1][:, PASSES * (e - 1) + s, :]).bitcast(FP4X4),
                 lhsT_scale=w_scale_rows[:, PASSES * e + s, :],
                 rhs=codes[s][:, C * e : C * (e + 1)].bitcast(FP8X4),
                 rhs_scale=scales[s][:, C * e : C * (e + 1)],
-                start=(s == 0),
-                stop=(s == PASSES - 1),
+                start=start,
+                stop=stop,
             )
+
+        def own_pass(bank, e, s, start, stop):
+            expert_pass(bank, own_codes, own_scales, e, s, start, stop)
 
         def load_far_words(s):
             nc.sync.dma_start(out=far_words[s][:], in_=x_words[s].rearrange("p t d -> p (t d)").bitcast(I32))
 
-        def gather_far_words(s, e0, e1):
-            nc.vector.tensor_copy(
-                far_codes[s][:, C * e0 : C * e1],
-                far_words[s][:].bitcast(U32).indirect(far_list[:, COLS_PER_EXPERT * e0 : COLS_PER_EXPERT * e1]),
-            )
+        def gather_far_words(s, a, b):
+            nc.vector.tensor_copy(far_codes[s][:, a:b], far_words[s][:].bitcast(U32).indirect(far_offsets(a, b)))
+
+        def gate_product(e):
+            nc.vector.tensor_tensor(gated[e][:], y_sb[e][:], gates[0][:, C * e : C * (e + 1)], MULT)
+
+        def scalar_scatter(e):
+            nc.scalar.activation(own[:].indirect(own_offsets(C * e, C * (e + 1))), gated[e][:], COPY)
 
         nc.vector.memset(far_scale_rows[:].bitcast(I32), 0)
         nc.vector.memset(warm_in[:], 0.0)
         nc.vector.memset(w_scale_rows[:].rearrange("p g n -> p (g n)").bitcast(I32), 0)
         nc.vector.memset(far_scales[1][:].bitcast(I32), 0)
         nc.vector.memset(own[:], 0.0)
+        nc.scalar.activation(warm_out[:], warm_in[:], GELU)
 
-        load_far_words(0)
-        nc.sync.dma_start(far_list[:], offs2)
-        gather_far_words(0, 0, E)
+        load_row(0)
         nc.sync.dma_start(own_list[:], offs)
+        load_row(1)
+        nc.sync.dma_start(far_list[:], offs2)
+        load_row(2)
         x_rows = x_scales.rearrange("s (q r) t -> r q s t", r=4)
         for r in range(4):
             nc.sync.dma_start(out=far_scale_rows[r:P:16, :].bitcast(I32), in_=x_rows[r].bitcast(I32))
-        nc.scalar.activation(warm_out[:], warm_in[:], GELU)
-        nc.vector.tensor_copy(far_scales[0][:], far_scale_rows[:].indirect(far_list[:]))
-
-        load_pair(0)
-        gather_pair(0, 0, E)
-        load_pair(1)
-        halves = [(0, 2), (2, 4)]
-        for e0, e1 in halves:
-            gather_pair(1, e0, e1)
-        for e0, e1 in halves:
-            interleave(nc.vector.tensor_copy, 0, e0, e1)
-        load_pair(2)
-        for e0, e1 in halves:
-            quantise(0, e0, e1)
-        words = pair2_and_last_row[:].bitcast(U32)
-        nc.vector.tensor_copy(woven[:].bitcast(U32)[:, :EARLY, 0], words[:, :T].indirect(offsets(0, EARLY)))
-        for j in range(2):
-            if j == 0:
-                nc.sync.dma_start(out=rows[j][:], in_=xo_pairs[1][1][:, j, :])
-                nc.gpsimd.tensor_scalar(planes[j][:, :ROUND_SPLIT], rows[j][:, :ROUND_SPLIT], 1.0, 0.0, MULT, ADD)
-                nc.scalar.copy(planes[j][:, ROUND_SPLIT:], rows[j][:, ROUND_SPLIT:])
-            else:
-                for c0, c1 in [(LAST_CUT, T), (0, LAST_CUT)]:
-                    nc.sync.dma_start(out=rows[j][:, c0:c1], in_=xo_pairs[1][1][:, j, c0:c1])
-                    nc.gpsimd.tensor_scalar(planes[j][:, c0:c1], rows[j][:, c0:c1], 1.0, 0.0, MULT, ADD)
+        for j in range(3, 8):
+            load_row(j)
         w_rows = w_scales.rearrange("e s (q r) n -> r q (e s) n", r=4)
         for r in range(4):
             nc.sync.dma_start(out=w_scale_rows[r:P:32, :, :].bitcast(I32), in_=w_rows[r].bitcast(I32))
-
         w_view = w_words.rearrange("e s p b -> p (e s) b").bitcast(I32)
-        nc.sync.dma_start(out=w_codes[:].bitcast(I32), in_=w_view)
-        far_words.append(sbuf("far_words1", [P, Q], I32))
+        nc.sync.dma_start(out=w_codes[0][:].bitcast(I32), in_=w_view[:, :PASSES, :])
+        nc.sync.dma_start(out=w_codes[1][:].bitcast(I32), in_=w_view[:, PASSES:, :])
+        nc.sync.dma_start(out=gates[0][:], in_=gate[:, : 2 * C])
+        load_far_words(0)
         load_far_words(1)
-        gate_sb = sbuf("gate_sb", [P, SLOTS], F32)
-        nc.sync.dma_start(out=gate_sb[:], in_=gate)
-        nc.sync.dma_start(out=far_scales[1][0 : P - 16, :].bitcast(I32), in_=far_scales[0][16:P, :].bitcast(I32))
+        nc.sync.dma_start(out=gates[1][:], in_=gate[:, 2 * C :])
 
-        for j in range(2):
-            nc.vector.tensor_copy(woven[:, :SPLIT, 2 + j], rows[j][:, :].indirect(offsets(0, SPLIT)))
-            for a, b in SCALAR_PIECES[j]:
-                nc.scalar.activation(woven[:, a:b, 2 + j], planes[j][:].indirect(offsets(a, b)), COPY)
-        nc.vector.tensor_copy(woven[:].bitcast(U32)[:, EARLY:, 0], words[:, : T + 16].indirect(offsets(EARLY, SLOTS)))
+        scalar_pick(0, 0, SLOTS)
+        vector_pick(1, 0, SLOTS)
+        scalar_pick(2, 0, SLOTS)
+        nc.vector.tensor_copy(far_scales[0][:], far_scale_rows[:].indirect(far_list[:]))
+        nc.sync.dma_start(out=far_scales[1][0 : P - 16, :].bitcast(I32), in_=far_scales[0][16:P, :].bitcast(I32))
+        scalar_pick(3, 0, 2 * C)
+        vector_pick(3, 2 * C, SLOTS)
+        for h in range(2):
+            weave(0, 2 * C * h, 2 * C * (h + 1))
+        for h in range(2):
+            quantise(0, 2 * C * h, 2 * C * (h + 1))
+        scalar_pick(4, 0, SLOTS)
+        scalar_pick(5, 0, 3 * C)
+        vector_pick(5, 3 * C, SLOTS)
+        scalar_pick(6, C, SLOTS)
+        vector_pick_woven(6, 0, C)
+        weave(1, 0, C, 2)
+        vector_pick_woven(7, 0, C)
+        for e in range(1, E):
+            scalar_pick(7, C * e, C * (e + 1))
+        own_pass(y_banks[0][:], 0, 0, True, False)
+
+        weave(1, C, 2 * C)
+        quantise(1, 0, C)
+        own_pass(y_banks[0][:], 0, 1, False, True)
+        nc.scalar.activation(y_sb[0][:], y_banks[0][:], GELU)
+        weave(1, 2 * C, 3 * C)
+        quantise(1, C, 2 * C)
+        own_pass(y_banks[1][:], 1, 1, True, False)
+        own_pass(y_banks[1][:], 1, 0, False, True)
+        nc.scalar.activation(y_sb[1][:], y_banks[1][:], GELU)
+        weave(1, 3 * C, 4 * C)
+        quantise(1, 2 * C, 3 * C)
+        own_pass(y_banks[2][:, :C], 2, 1, True, False)
+        own_pass(y_banks[2][:, :C], 2, 0, False, False)
+        own_pass(y_banks[2][:, C:], 3, 0, False, False)
+        gate_product(0)
+        scalar_scatter(0)
+        quantise(1, 3 * C, 4 * C)
+        own_pass(y_banks[2][:, C:], 3, 1, False, True)
+        y_last = sbuf("y_last", [P, 2 * C], F32, tag="gated0")
+        nc.scalar.activation(y_last[:], y_banks[2][:], GELU)
+        gate_product(1)
+        scalar_scatter(1)
+
+        far_codes = [sbuf("far_codes0", [P, SLOTS], U32, tag="y1"), sbuf("far_codes1", [P, SLOTS], U32)]
+        gather_far_words(0, 0, SLOTS)
         for e in range(E):
-            expert_pass(y_banks[e][:], own_codes, own_scales, e, 0)
-        for e0, e1 in [(0, 1), (1, 3), (3, 4)]:
-            quantise(1, e0, e1)
-            for e in range(e0, e1):
-                expert_pass(y_banks[e][:], own_codes, own_scales, e, 1)
-                nc.scalar.activation(y_sb[:, C * e : C * (e + 1)], y_banks[e][:], GELU)
-        far_codes.append(sbuf("far_codes1", [P, SLOTS], U32, tag="woven"))
-        gather_far_words(1, 0, E)
-        z_bank = psum.tile([P, SLOTS], F32, name="z_bank", tag=f"y_bank{E - 1}")
-        for e in range(E):
-            for s in range(PASSES):
-                expert_pass(z_bank[:, C * e : C * (e + 1)], far_codes, far_scales, e, s)
-        nc.scalar.activation(z_sb[:], z_bank[:], GELU)
+            expert_pass(z_banks[e // 2][:, C * (e % 2) : C * (e % 2 + 1)], far_codes, far_scales, e, 0, e % 2 == 0, False)
+        for h in range(2):
+            gather_far_words(1, 2 * C * h, 2 * C * (h + 1))
+            for e in (2 * h, 2 * h + 1):
+                expert_pass(z_banks[h][:, C * (e % 2) : C * (e % 2 + 1)], far_codes, far_scales, e, 1, False, e % 2 == 1)
+            nc.scalar.activation(z_sb[:, 2 * C * h : 2 * C * (h + 1)], z_banks[h][:], GELU)
+        nc.vector.tensor_tensor(own[:].indirect(own_offsets(2 * C, 4 * C)), y_last[:], gates[1][:], MULT)
         nc.scalar.dma_start(out=out[:, T:], in_=z_sb[:])
-        nc.vector.tensor_tensor(own[:].indirect(own_list[:]), y_sb[:], gate_sb[:], MULT)
         nc.sync.dma_start(out=out[:, :T], in_=own[:])

@@ -1,6 +1,7 @@
 from contextlib import ExitStack
 
 import concourse.mybir as mybir
+from concourse.masks import make_identity
 
 K, T, Q, E, C, N = 1024, 1024, 1024, 4, 128, 128
 P = 128
@@ -36,23 +37,32 @@ def tile_moe_loc_lin_gelu_kernel(tc, x_words, x_scales, xo, w_words, w_scales, g
         far_list = keep.tile([P, LIST_COLS], U16, name="far_list")
         far_scale_rows = sbuf("far_scale_rows", [P, Q], U8)
         w_scale_rows = sbuf("w_scale_rows", [P, E * PASSES, N], U8)
-        w_codes = [sbuf("w_first", [P, PASSES, 2 * N], U8), sbuf("w_rest", [P, (E - 1) * PASSES, 2 * N], U8)]
+        w_codes = [sbuf("w0", [P, PASSES, 2 * N], U8), sbuf("w1", [P, PASSES, 2 * N], U8), sbuf("w23", [P, 2 * PASSES, 2 * N], U8)]
         far_words = [sbuf(f"far_words{s}", [P, Q], I32) for s in range(PASSES)]
         far_scales = [sbuf(f"far_scales{s}", [P, SLOTS], U8) for s in range(PASSES)]
         rows = [sbuf(f"row{j}", [P, T], F32) for j in range(8)]
-        picked = [sbuf(f"picked{s}", [P, 4, SLOTS], BF16) for s in range(PASSES)]
+        picked0 = sbuf("picked0", [P, 4, SLOTS], BF16)
+        picked1 = sbuf("picked1", [P, 4, 3 * C], BF16)
+        picked_last = sbuf("picked_last", [P, 4, C], BF16)
+
+        def picked(s, a, b):
+            if s == 0:
+                return picked0[:, :, a:b]
+            return picked1[:, :, a:b] if a < 3 * C else picked_last[:, :, a - 3 * C : b - 3 * C]
+
         woven = [sbuf(f"woven{s}", [P, SLOTS, 4], BF16) for s in range(PASSES)]
-        own_codes = [sbuf(f"own_codes{s}", [P, SLOTS], U32) for s in range(PASSES)]
+        own_codes = {}
         own_scales = [sbuf(f"own_scales{s}", [P, SLOTS], U8) for s in range(PASSES)]
         y_sb = [sbuf(f"y{e}", [P, C], F32) for e in range(2)]
-        gated = [sbuf(f"gated{e}", [P, C], F32) for e in range(2)]
         z_sb = sbuf("z_sb", [P, SLOTS], F32)
         gates = [sbuf(f"gate{h}", [P, 2 * C], F32) for h in range(2)]
+        gate_row = sbuf("gate_row", [P, 2], F32)
+        identity = sbuf("identity", [P, P], F32)
+        gate_bank = psum.tile([P, 2, P], F32, name="gate_bank")
         own = sbuf("own", [P, T], F32)
         warm_in = sbuf("warm_in", [P, 8], F32)
         warm_out = sbuf("warm_out", [P, 8], F32)
         y_banks = [psum.tile([P, C], F32, name="y_bank0"), psum.tile([P, C], F32, name="y_bank1"), psum.tile([P, 2 * C], F32, name="y_bank23")]
-        z_banks = [psum.tile([P, 2 * C], F32, name=f"z_bank{h}") for h in range(2)]
 
         xo_rows = xo.rearrange("(s p t) c -> s t p c", s=PASSES, p=P, t=4)
 
@@ -66,20 +76,23 @@ def tile_moe_loc_lin_gelu_kernel(tc, x_words, x_scales, xo, w_words, w_scales, g
             nc.sync.dma_start(out=rows[j][:], in_=xo_rows[j // 4][j % 4])
 
         def scalar_pick(j, a, b):
-            nc.scalar.activation(picked[j // 4][:, j % 4, a:b], rows[j][:].indirect(own_offsets(a, b)), COPY)
+            nc.scalar.activation(picked(j // 4, a, b)[:, j % 4, :], rows[j][:].indirect(own_offsets(a, b)), COPY)
 
         def vector_pick(j, a, b):
-            nc.vector.tensor_copy(picked[j // 4][:, j % 4, a:b], rows[j][:].indirect(own_offsets(a, b)))
+            nc.vector.tensor_copy(picked(j // 4, a, b)[:, j % 4, :], rows[j][:].indirect(own_offsets(a, b)))
 
         def vector_pick_woven(j, a, b):
             nc.vector.tensor_copy(woven[j // 4][:, a:b, j % 4], rows[j][:].indirect(own_offsets(a, b)))
 
         def weave(s, a, b, count=4):
-            nc.vector.tensor_copy(woven[s][:, a:b, :count], picked[s][:, :count, a:b].rearrange("p t c -> p c t"))
+            nc.vector.tensor_copy(woven[s][:, a:b, :count], picked(s, a, b)[:, :count, :].rearrange("p t c -> p c t"))
 
-        def quantise(s, a, b):
+        def quantise(s, a, b, tag=None):
+            codes = sbuf(f"own_codes{s}_{a}", [P, b - a], U32, tag=tag)
+            for e in range(a // C, b // C):
+                own_codes[(s, e)] = codes[:, C * e - a : C * (e + 1) - a]
             nc.vector.quantize_mx(
-                out=own_codes[s][:, a:b].bitcast(FP8X4),
+                out=codes[:].bitcast(FP8X4),
                 scales=own_scales[s][:, a:b],
                 in_=woven[s][:, a:b, :].rearrange("p c t -> p (c t)"),
             )
@@ -87,16 +100,16 @@ def tile_moe_loc_lin_gelu_kernel(tc, x_words, x_scales, xo, w_words, w_scales, g
         def expert_pass(bank, codes, scales, e, s, start, stop):
             nc.tensor.matmul_mx(
                 out=bank,
-                lhsT=(w_codes[0][:, s, :] if e == 0 else w_codes[1][:, PASSES * (e - 1) + s, :]).bitcast(FP4X4),
+                lhsT=(w_codes[e][:, s, :] if e < 2 else w_codes[2][:, PASSES * (e - 2) + s, :]).bitcast(FP4X4),
                 lhsT_scale=w_scale_rows[:, PASSES * e + s, :],
-                rhs=codes[s][:, C * e : C * (e + 1)].bitcast(FP8X4),
+                rhs=codes.bitcast(FP8X4),
                 rhs_scale=scales[s][:, C * e : C * (e + 1)],
                 start=start,
                 stop=stop,
             )
 
         def own_pass(bank, e, s, start, stop):
-            expert_pass(bank, own_codes, own_scales, e, s, start, stop)
+            expert_pass(bank, own_codes[(s, e)], own_scales, e, s, start, stop)
 
         def load_far_words(s):
             nc.sync.dma_start(out=far_words[s][:], in_=x_words[s].rearrange("p t d -> p (t d)").bitcast(I32))
@@ -119,6 +132,11 @@ def tile_moe_loc_lin_gelu_kernel(tc, x_words, x_scales, xo, w_words, w_scales, g
 
         load_row(0)
         nc.sync.dma_start(own_list[:], offs)
+        nc.sync.dma_start(out=gate_row[:], in_=gate[0, : 2 * C].rearrange("(p f) -> p f", f=2))
+        make_identity(nc, identity[:])
+        for f in range(2):
+            nc.tensor.transpose(gate_bank[:, f, :], gate_row[:, f : f + 1].to_broadcast([P, P]), identity[:])
+        nc.vector.tensor_copy(gates[0][:].rearrange("n (p f) -> n p f", f=2), gate_bank[:].rearrange("n f p -> n p f"))
         load_row(1)
         nc.sync.dma_start(far_list[:], offs2)
         load_row(2)
@@ -131,10 +149,10 @@ def tile_moe_loc_lin_gelu_kernel(tc, x_words, x_scales, xo, w_words, w_scales, g
         for r in range(4):
             nc.sync.dma_start(out=w_scale_rows[r:P:32, :, :].bitcast(I32), in_=w_rows[r].bitcast(I32))
         w_view = w_words.rearrange("e s p b -> p (e s) b").bitcast(I32)
-        nc.sync.dma_start(out=w_codes[0][:].bitcast(I32), in_=w_view[:, :PASSES, :])
-        nc.sync.dma_start(out=w_codes[1][:].bitcast(I32), in_=w_view[:, PASSES:, :])
-        nc.sync.dma_start(out=gates[0][:], in_=gate[:, : 2 * C])
+        for e in range(2):
+            nc.sync.dma_start(out=w_codes[e][:].bitcast(I32), in_=w_view[:, PASSES * e : PASSES * (e + 1), :])
         load_far_words(0)
+        nc.sync.dma_start(out=w_codes[2][:].bitcast(I32), in_=w_view[:, 2 * PASSES :, :])
         load_far_words(1)
         nc.sync.dma_start(out=gates[1][:], in_=gate[:, 2 * C :])
 
@@ -149,49 +167,57 @@ def tile_moe_loc_lin_gelu_kernel(tc, x_words, x_scales, xo, w_words, w_scales, g
             weave(0, 2 * C * h, 2 * C * (h + 1))
         for h in range(2):
             quantise(0, 2 * C * h, 2 * C * (h + 1))
-        scalar_pick(4, 0, SLOTS)
+        scalar_pick(4, 0, 3 * C)
+        scalar_pick(4, 3 * C, SLOTS)
         scalar_pick(5, 0, 3 * C)
         vector_pick(5, 3 * C, SLOTS)
-        scalar_pick(6, C, SLOTS)
+        scalar_pick(6, C, 3 * C)
+        scalar_pick(6, 3 * C, SLOTS)
         vector_pick_woven(6, 0, C)
         weave(1, 0, C, 2)
         vector_pick_woven(7, 0, C)
-        for e in range(1, E):
+        vector_pick(7, 3 * C, SLOTS)
+        for e in range(1, 3):
             scalar_pick(7, C * e, C * (e + 1))
+        nc.scalar.copy(woven[1][:, 3 * C :, :], picked_last[:].rearrange("p t c -> p c t"))
         own_pass(y_banks[0][:], 0, 0, True, False)
+        own_pass(y_banks[1][:], 1, 0, True, False)
 
-        weave(1, C, 2 * C)
         quantise(1, 0, C)
+        weave(1, C, 2 * C)
         own_pass(y_banks[0][:], 0, 1, False, True)
         nc.scalar.activation(y_sb[0][:], y_banks[0][:], GELU)
         weave(1, 2 * C, 3 * C)
-        quantise(1, C, 2 * C)
-        own_pass(y_banks[1][:], 1, 1, True, False)
-        own_pass(y_banks[1][:], 1, 0, False, True)
+        quantise(1, C, 2 * C, tag="picked1")
+        own_pass(y_banks[1][:], 1, 1, False, True)
         nc.scalar.activation(y_sb[1][:], y_banks[1][:], GELU)
-        weave(1, 3 * C, 4 * C)
-        quantise(1, 2 * C, 3 * C)
+        gated = [sbuf("gated0", [P, C], F32, tag="picked_last"), sbuf("gated1", [P, C], F32)]
+        gate_product(0)
+        scalar_scatter(0)
+        quantise(1, 2 * C, 4 * C, tag="y0")
         own_pass(y_banks[2][:, :C], 2, 1, True, False)
         own_pass(y_banks[2][:, :C], 2, 0, False, False)
         own_pass(y_banks[2][:, C:], 3, 0, False, False)
-        gate_product(0)
-        scalar_scatter(0)
-        quantise(1, 3 * C, 4 * C)
         own_pass(y_banks[2][:, C:], 3, 1, False, True)
-        y_last = sbuf("y_last", [P, 2 * C], F32, tag="gated0")
+        y_last = sbuf("y_last", [P, 2 * C], F32, tag="picked_last")
         nc.scalar.activation(y_last[:], y_banks[2][:], GELU)
-        gate_product(1)
+        nc.gpsimd.tensor_tensor(gated[1][:], y_sb[1][:], gates[0][:, C:], MULT)
         scalar_scatter(1)
 
-        far_codes = [sbuf("far_codes0", [P, SLOTS], U32, tag="y1"), sbuf("far_codes1", [P, SLOTS], U32)]
+        far_codes = [sbuf("far_codes0", [P, SLOTS], U32, tag="woven1"), sbuf("far_codes1", [P, SLOTS], U32)]
+        z_banks = [psum.tile([P, 3 * C], F32, name="z_bank0"), psum.tile([P, C], F32, name="z_bank1")]
         gather_far_words(0, 0, SLOTS)
-        for e in range(E):
-            expert_pass(z_banks[e // 2][:, C * (e % 2) : C * (e % 2 + 1)], far_codes, far_scales, e, 0, e % 2 == 0, False)
-        for h in range(2):
-            gather_far_words(1, 2 * C * h, 2 * C * (h + 1))
-            for e in (2 * h, 2 * h + 1):
-                expert_pass(z_banks[h][:, C * (e % 2) : C * (e % 2 + 1)], far_codes, far_scales, e, 1, False, e % 2 == 1)
-            nc.scalar.activation(z_sb[:, 2 * C * h : 2 * C * (h + 1)], z_banks[h][:], GELU)
+
+        def far_pass(e, s, start, stop):
+            expert_pass(z_banks[e // 3][:, C * (e % 3) : C * (e % 3 + 1)], far_codes[s][:, C * e : C * (e + 1)], far_scales, e, s, start, stop)
+
+        for e in (2, 0, 1, 3):
+            far_pass(e, 0, e >= 2, False)
+        for h, (e0, e1) in enumerate([(0, 3), (3, 4)]):
+            gather_far_words(1, C * e0, C * e1)
+            for e in range(e0, e1):
+                far_pass(e, 1, False, e == e1 - 1)
+            nc.scalar.activation(z_sb[:, C * e0 : C * e1], z_banks[h][:], GELU)
         nc.vector.tensor_tensor(own[:].indirect(own_offsets(2 * C, 4 * C)), y_last[:], gates[1][:], MULT)
         nc.scalar.dma_start(out=out[:, T:], in_=z_sb[:])
         nc.sync.dma_start(out=out[:, :T], in_=own[:])

@@ -143,11 +143,13 @@ def tile_moe_loc_lin_gelu_kernel(tc, x_words, x_scales, xo, w_words, w_scales, g
         x_rows = x_scales.rearrange("s (q r) t -> r q s t", r=4)
         for r in range(4):
             nc.sync.dma_start(out=far_scale_rows[r:P:16, :].bitcast(I32), in_=x_rows[r].bitcast(I32))
-        for j in range(3, 8):
+        load_row(3)
+        nc.sync.dma_start(out=w_scale_rows[:16, :, :].bitcast(I32), in_=w_scales.rearrange("e s b n -> b (e s) n").bitcast(I32))
+        for j in range(4, 8):
             load_row(j)
-        w_rows = w_scales.rearrange("e s (q r) n -> r q (e s) n", r=4)
-        for r in range(4):
-            nc.sync.dma_start(out=w_scale_rows[r:P:32, :, :].bitcast(I32), in_=w_rows[r].bitcast(I32))
+        w_scale_words = w_scale_rows[:].rearrange("p g n -> p (g n)").bitcast(I32)
+        for q in range(1, 4):
+            nc.sync.dma_start(out=w_scale_words[32 * q : 32 * q + 4, :], in_=w_scale_words[4 * q : 4 * q + 4, :])
         w_view = w_words.rearrange("e s p b -> p (e s) b").bitcast(I32)
         for e in range(2):
             nc.sync.dma_start(out=w_codes[e][:].bitcast(I32), in_=w_view[:, PASSES * e : PASSES * (e + 1), :])

@@ -1,7 +1,6 @@
 from contextlib import ExitStack
 
 import concourse.mybir as mybir
-from concourse.masks import make_identity
 
 K, T, Q, E, C, N = 1024, 1024, 1024, 4, 128, 128
 P = 128
@@ -37,7 +36,7 @@ def tile_moe_loc_lin_gelu_kernel(tc, x_words, x_scales, xo, w_words, w_scales, g
         far_list = keep.tile([P, LIST_COLS], U16, name="far_list")
         far_scale_rows = sbuf("far_scale_rows", [P, Q], U8)
         w_scale_rows = sbuf("w_scale_rows", [P, E * PASSES, N], U8)
-        w_codes = [sbuf("w0", [P, PASSES, 2 * N], U8), sbuf("w1", [P, PASSES, 2 * N], U8), sbuf("w23", [P, 2 * PASSES, 2 * N], U8)]
+        w_codes = [sbuf("w_first", [P, PASSES, 2 * N], U8), sbuf("w_rest", [P, 3 * PASSES, 2 * N], U8)]
         far_words = [sbuf(f"far_words{s}", [P, Q], I32) for s in range(PASSES)]
         far_scales = [sbuf(f"far_scales{s}", [P, SLOTS], U8) for s in range(PASSES)]
         rows = [sbuf(f"row{j}", [P, T], F32) for j in range(8)]
@@ -53,16 +52,14 @@ def tile_moe_loc_lin_gelu_kernel(tc, x_words, x_scales, xo, w_words, w_scales, g
         woven = [sbuf(f"woven{s}", [P, SLOTS, 4], BF16) for s in range(PASSES)]
         own_codes = {}
         own_scales = [sbuf(f"own_scales{s}", [P, SLOTS], U8) for s in range(PASSES)]
-        y_sb = [sbuf(f"y{e}", [P, C], F32) for e in range(2)]
+        y_first = sbuf("y_first", [P, C], F32)
         z_sb = sbuf("z_sb", [P, SLOTS], F32)
-        gates = [sbuf(f"gate{h}", [P, 2 * C], F32) for h in range(2)]
-        gate_row = sbuf("gate_row", [P, 2], F32)
-        identity = sbuf("identity", [P, P], F32)
-        gate_bank = psum.tile([P, 2, P], F32, name="gate_bank")
+        gate_first = sbuf("gate_first", [P, C], F32)
+        gate_rest = sbuf("gate_rest", [P, 3 * C], F32)
         own = sbuf("own", [P, T], F32)
         warm_in = sbuf("warm_in", [P, 8], F32)
         warm_out = sbuf("warm_out", [P, 8], F32)
-        y_banks = [psum.tile([P, C], F32, name="y_bank0"), psum.tile([P, C], F32, name="y_bank1"), psum.tile([P, 2 * C], F32, name="y_bank23")]
+        y_banks = [psum.tile([P, C], F32, name="y_bank_first"), psum.tile([P, 3 * C], F32, name="y_bank_rest")]
 
         xo_rows = xo.rearrange("(s p t) c -> s t p c", s=PASSES, p=P, t=4)
 
@@ -100,7 +97,7 @@ def tile_moe_loc_lin_gelu_kernel(tc, x_words, x_scales, xo, w_words, w_scales, g
         def expert_pass(bank, codes, scales, e, s, start, stop):
             nc.tensor.matmul_mx(
                 out=bank,
-                lhsT=(w_codes[e][:, s, :] if e < 2 else w_codes[2][:, PASSES * (e - 2) + s, :]).bitcast(FP4X4),
+                lhsT=(w_codes[0][:, s, :] if e == 0 else w_codes[1][:, PASSES * (e - 1) + s, :]).bitcast(FP4X4),
                 lhsT_scale=w_scale_rows[:, PASSES * e + s, :],
                 rhs=codes.bitcast(FP8X4),
                 rhs_scale=scales[s][:, C * e : C * (e + 1)],
@@ -117,12 +114,6 @@ def tile_moe_loc_lin_gelu_kernel(tc, x_words, x_scales, xo, w_words, w_scales, g
         def gather_far_words(s, a, b):
             nc.vector.tensor_copy(far_codes[s][:, a:b], far_words[s][:].bitcast(U32).indirect(far_offsets(a, b)))
 
-        def gate_product(e):
-            nc.vector.tensor_tensor(gated[e][:], y_sb[e][:], gates[0][:, C * e : C * (e + 1)], MULT)
-
-        def scalar_scatter(e):
-            nc.scalar.activation(own[:].indirect(own_offsets(C * e, C * (e + 1))), gated[e][:], COPY)
-
         nc.vector.memset(far_scale_rows[:].bitcast(I32), 0)
         nc.vector.memset(warm_in[:], 0.0)
         nc.vector.memset(w_scale_rows[:].rearrange("p g n -> p (g n)").bitcast(I32), 0)
@@ -132,11 +123,6 @@ def tile_moe_loc_lin_gelu_kernel(tc, x_words, x_scales, xo, w_words, w_scales, g
 
         load_row(0)
         nc.sync.dma_start(own_list[:], offs)
-        nc.sync.dma_start(out=gate_row[:], in_=gate[0, : 2 * C].rearrange("(p f) -> p f", f=2))
-        make_identity(nc, identity[:])
-        for f in range(2):
-            nc.tensor.transpose(gate_bank[:, f, :], gate_row[:, f : f + 1].to_broadcast([P, P]), identity[:])
-        nc.vector.tensor_copy(gates[0][:].rearrange("n (p f) -> n p f", f=2), gate_bank[:].rearrange("n f p -> n p f"))
         load_row(1)
         nc.sync.dma_start(far_list[:], offs2)
         load_row(2)
@@ -151,12 +137,12 @@ def tile_moe_loc_lin_gelu_kernel(tc, x_words, x_scales, xo, w_words, w_scales, g
         for q in range(1, 4):
             nc.sync.dma_start(out=w_scale_words[32 * q : 32 * q + 4, :], in_=w_scale_words[4 * q : 4 * q + 4, :])
         w_view = w_words.rearrange("e s p b -> p (e s) b").bitcast(I32)
-        for e in range(2):
-            nc.sync.dma_start(out=w_codes[e][:].bitcast(I32), in_=w_view[:, PASSES * e : PASSES * (e + 1), :])
+        nc.sync.dma_start(out=w_codes[0][:].bitcast(I32), in_=w_view[:, :PASSES, :])
         load_far_words(0)
-        nc.sync.dma_start(out=w_codes[2][:].bitcast(I32), in_=w_view[:, 2 * PASSES :, :])
+        nc.sync.dma_start(out=gate_first[:], in_=gate[:, :C])
+        nc.sync.dma_start(out=w_codes[1][:].bitcast(I32), in_=w_view[:, PASSES:, :])
         load_far_words(1)
-        nc.sync.dma_start(out=gates[1][:], in_=gate[:, 2 * C :])
+        nc.sync.dma_start(out=gate_rest[:], in_=gate[:, C:])
 
         scalar_pick(0, 0, SLOTS)
         vector_pick(1, 0, SLOTS)
@@ -183,43 +169,30 @@ def tile_moe_loc_lin_gelu_kernel(tc, x_words, x_scales, xo, w_words, w_scales, g
             scalar_pick(7, C * e, C * (e + 1))
         nc.scalar.copy(woven[1][:, 3 * C :, :], picked_last[:].rearrange("p t c -> p c t"))
         own_pass(y_banks[0][:], 0, 0, True, False)
-        own_pass(y_banks[1][:], 1, 0, True, False)
 
         quantise(1, 0, C)
         weave(1, C, 2 * C)
         own_pass(y_banks[0][:], 0, 1, False, True)
-        nc.scalar.activation(y_sb[0][:], y_banks[0][:], GELU)
+        nc.scalar.activation(y_first[:], y_banks[0][:], GELU)
         weave(1, 2 * C, 3 * C)
         quantise(1, C, 2 * C, tag="picked1")
-        own_pass(y_banks[1][:], 1, 1, False, True)
-        nc.scalar.activation(y_sb[1][:], y_banks[1][:], GELU)
-        gated = [sbuf("gated0", [P, C], F32, tag="picked_last"), sbuf("gated1", [P, C], F32)]
-        gate_product(0)
-        scalar_scatter(0)
-        quantise(1, 2 * C, 4 * C, tag="y0")
-        own_pass(y_banks[2][:, :C], 2, 1, True, False)
-        own_pass(y_banks[2][:, :C], 2, 0, False, False)
-        own_pass(y_banks[2][:, C:], 3, 0, False, False)
-        own_pass(y_banks[2][:, C:], 3, 1, False, True)
-        y_last = sbuf("y_last", [P, 2 * C], F32, tag="picked_last")
-        nc.scalar.activation(y_last[:], y_banks[2][:], GELU)
-        nc.gpsimd.tensor_tensor(gated[1][:], y_sb[1][:], gates[0][:, C:], MULT)
-        scalar_scatter(1)
+        quantise(1, 2 * C, 4 * C)
+        gated = sbuf("gated", [P, C], F32, tag="picked_last")
+        nc.gpsimd.tensor_tensor(gated[:], y_first[:], gate_first[:], MULT)
+        nc.scalar.activation(own[:].indirect(own_offsets(0, C)), gated[:], COPY)
+        for s in range(PASSES):
+            for e in range(1, E):
+                own_pass(y_banks[1][:, C * (e - 1) : C * e], e, s, (s, e) == (0, 1), (s, e) == (1, E - 1))
+        y_rest = sbuf("y_rest", [P, 3 * C], F32, tag="picked_last")
+        nc.scalar.activation(y_rest[:], y_banks[1][:], GELU)
 
         far_codes = [sbuf("far_codes0", [P, SLOTS], U32, tag="woven1"), sbuf("far_codes1", [P, SLOTS], U32)]
-        z_banks = [psum.tile([P, 3 * C], F32, name="z_bank0"), psum.tile([P, C], F32, name="z_bank1")]
-        gather_far_words(0, 0, SLOTS)
-
-        def far_pass(e, s, start, stop):
-            expert_pass(z_banks[e // 3][:, C * (e % 3) : C * (e % 3 + 1)], far_codes[s][:, C * e : C * (e + 1)], far_scales, e, s, start, stop)
-
-        for e in (2, 0, 1, 3):
-            far_pass(e, 0, e >= 2, False)
-        for h, (e0, e1) in enumerate([(0, 3), (3, 4)]):
-            gather_far_words(1, C * e0, C * e1)
-            for e in range(e0, e1):
-                far_pass(e, 1, False, e == e1 - 1)
-            nc.scalar.activation(z_sb[:, C * e0 : C * e1], z_banks[h][:], GELU)
-        nc.vector.tensor_tensor(own[:].indirect(own_offsets(2 * C, 4 * C)), y_last[:], gates[1][:], MULT)
+        z_bank = psum.tile([P, SLOTS], F32, name="z_bank")
+        for s in range(PASSES):
+            gather_far_words(s, 0, SLOTS)
+            for e in (3, 2, 1, 0):
+                expert_pass(z_bank[:, C * e : C * (e + 1)], far_codes[s][:, C * e : C * (e + 1)], far_scales, e, s, (s, e) == (0, 3), (s, e) == (1, 0))
+        nc.scalar.activation(z_sb[:], z_bank[:], GELU)
+        nc.vector.tensor_tensor(own[:].indirect(own_offsets(C, SLOTS)), y_rest[:], gate_rest[:], MULT)
         nc.scalar.dma_start(out=out[:, T:], in_=z_sb[:])
         nc.sync.dma_start(out=out[:, :T], in_=own[:])

@@ -39,8 +39,9 @@ def tile_moe_loc_lin_gelu_kernel(tc, x_words, x_scales, xo, w_words, w_scales, g
         w_codes = [sbuf("w_first", [P, PASSES, 2 * N], U8), sbuf("w_rest", [P, 3 * PASSES, 2 * N], U8)]
         far_words = [sbuf(f"far_words{s}", [P, Q], I32) for s in range(PASSES)]
         far_scales = [sbuf(f"far_scales{s}", [P, SLOTS], U8) for s in range(PASSES)]
-        rows = [sbuf(f"row{j}", [P, T], F32) for j in range(8)]
-        picked0 = sbuf("picked0", [P, 4, SLOTS], BF16)
+        row_pairs = [sbuf(f"row_pair{i}", [P, 2, T], F32) for i in range(2)]
+        rows = [row_pairs[j // 2][:, j % 2, :] for j in range(4)] + [sbuf(f"row{j}", [P, T], F32)[:] for j in range(4, 8)]
+        picked0 = sbuf("picked0", [P, 4, SLOTS], F32)
         picked1 = sbuf("picked1", [P, 4, 3 * C], BF16)
         picked_last = sbuf("picked_last", [P, 4, C], BF16)
 
@@ -70,16 +71,19 @@ def tile_moe_loc_lin_gelu_kernel(tc, x_words, x_scales, xo, w_words, w_scales, g
             return far_list[:, a // 16 : b // 16]
 
         def load_row(j):
-            nc.sync.dma_start(out=rows[j][:], in_=xo_rows[j // 4][j % 4])
+            nc.sync.dma_start(out=rows[j], in_=xo_rows[j // 4][j % 4])
+
+        def load_pair(i):
+            nc.sync.dma_start(out=row_pairs[i][:], in_=xo[: 4 * P].rearrange("(p u e) c -> u p e c", u=2, e=2)[i])
 
         def scalar_pick(j, a, b):
-            nc.scalar.activation(picked(j // 4, a, b)[:, j % 4, :], rows[j][:].indirect(own_offsets(a, b)), COPY)
+            nc.scalar.activation(picked(j // 4, a, b)[:, j % 4, :], rows[j].indirect(own_offsets(a, b)), COPY)
 
         def vector_pick(j, a, b):
-            nc.vector.tensor_copy(picked(j // 4, a, b)[:, j % 4, :], rows[j][:].indirect(own_offsets(a, b)))
+            nc.vector.tensor_copy(picked(j // 4, a, b)[:, j % 4, :], rows[j].indirect(own_offsets(a, b)))
 
         def vector_pick_woven(j, a, b):
-            nc.vector.tensor_copy(woven[j // 4][:, a:b, j % 4], rows[j][:].indirect(own_offsets(a, b)))
+            nc.vector.tensor_copy(woven[j // 4][:, a:b, j % 4], rows[j].indirect(own_offsets(a, b)))
 
         def weave(s, a, b, count=4):
             nc.vector.tensor_copy(woven[s][:, a:b, :count], picked(s, a, b)[:, :count, :].rearrange("p t c -> p c t"))
@@ -121,15 +125,13 @@ def tile_moe_loc_lin_gelu_kernel(tc, x_words, x_scales, xo, w_words, w_scales, g
         nc.vector.memset(own[:], 0.0)
         nc.scalar.activation(warm_out[:], warm_in[:], GELU)
 
-        load_row(0)
+        load_pair(0)
         nc.sync.dma_start(own_list[:], offs)
-        load_row(1)
         nc.sync.dma_start(far_list[:], offs2)
-        load_row(2)
         x_rows = x_scales.rearrange("s (q r) t -> r q s t", r=4)
         for r in range(4):
             nc.sync.dma_start(out=far_scale_rows[r:P:16, :].bitcast(I32), in_=x_rows[r].bitcast(I32))
-        load_row(3)
+        load_pair(1)
         nc.sync.dma_start(out=w_scale_rows[:16, :, :].bitcast(I32), in_=w_scales.rearrange("e s b n -> b (e s) n").bitcast(I32))
         for j in range(4, 8):
             load_row(j)
@@ -149,8 +151,8 @@ def tile_moe_loc_lin_gelu_kernel(tc, x_words, x_scales, xo, w_words, w_scales, g
         scalar_pick(2, 0, SLOTS)
         nc.vector.tensor_copy(far_scales[0][:], far_scale_rows[:].indirect(far_list[:]))
         nc.sync.dma_start(out=far_scales[1][0 : P - 16, :].bitcast(I32), in_=far_scales[0][16:P, :].bitcast(I32))
-        scalar_pick(3, 0, 2 * C)
-        vector_pick(3, 2 * C, SLOTS)
+        scalar_pick(3, 0, C)
+        vector_pick(3, C, SLOTS)
         for h in range(2):
             weave(0, 2 * C * h, 2 * C * (h + 1))
         for h in range(2):

@@ -147,12 +147,13 @@ def tile_moe_loc_lin_gelu_kernel(tc, x_words, x_scales, xo, w_words, w_scales, g
         nc.sync.dma_start(out=gate_rest[:], in_=gate[:, C:])
 
         scalar_pick(0, 0, SLOTS)
-        vector_pick(1, 0, SLOTS)
-        scalar_pick(2, 0, SLOTS)
+        scalar_pick(1, 0, 2 * C)
+        vector_pick(1, 2 * C, SLOTS)
         nc.vector.tensor_copy(far_scales[0][:], far_scale_rows[:].indirect(far_list[:]))
         nc.sync.dma_start(out=far_scales[1][0 : P - 16, :].bitcast(I32), in_=far_scales[0][16:P, :].bitcast(I32))
-        scalar_pick(3, 0, C)
-        vector_pick(3, C, SLOTS)
+        for h in range(2):
+            scalar_pick(2, 2 * C * h, 2 * C * (h + 1))
+            vector_pick(3, 2 * C * h, 2 * C * (h + 1))
         for h in range(2):
             weave(0, 2 * C * h, 2 * C * (h + 1))
         for h in range(2):

@@ -1,6 +1,7 @@
 from contextlib import ExitStack
 
 import concourse.mybir as mybir
+from concourse.masks import make_identity
 
 K, T, Q, E, C, N = 1024, 1024, 1024, 4, 128, 128
 P = 128
@@ -36,9 +37,10 @@ def tile_moe_loc_lin_gelu_kernel(tc, x_words, x_scales, xo, w_words, w_scales, g
         far_list = keep.tile([P, LIST_COLS], U16, name="far_list")
         far_scale_rows = sbuf("far_scale_rows", [P, Q], U8)
         w_scale_rows = sbuf("w_scale_rows", [P, E * PASSES, N], U8)
-        w_codes = [sbuf("w_first", [P, PASSES, 2 * N], U8), sbuf("w_rest", [P, 3 * PASSES, 2 * N], U8)]
+        w_codes = [sbuf(f"w_half{h}", [P, 2 * PASSES, 2 * N], U8) for h in range(2)]
         far_words = [sbuf(f"far_words{s}", [P, Q], I32) for s in range(PASSES)]
         far_scales = [sbuf(f"far_scales{s}", [P, SLOTS], U8) for s in range(PASSES)]
+        far_codes = [sbuf(f"far_codes{s}", [P, SLOTS], U32) for s in range(PASSES)]
         row_pairs = [sbuf(f"row_pair{i}", [P, 2, T], F32) for i in range(2)]
         rows = [row_pairs[j // 2][:, j % 2, :] for j in range(4)] + [sbuf(f"row{j}", [P, T], F32)[:] for j in range(4, 8)]
         picked0 = sbuf("picked0", [P, 4, SLOTS], F32)
@@ -51,30 +53,36 @@ def tile_moe_loc_lin_gelu_kernel(tc, x_words, x_scales, xo, w_words, w_scales, g
             return picked1[:, :, a:b] if a < 3 * C else picked_last[:, :, a - 3 * C : b - 3 * C]
 
         woven = [sbuf(f"woven{s}", [P, SLOTS, 4], BF16) for s in range(PASSES)]
-        own_codes = {}
+        own_codes = [sbuf(f"own_codes{s}", [P, SLOTS], U32) for s in range(PASSES)]
         own_scales = [sbuf(f"own_scales{s}", [P, SLOTS], U8) for s in range(PASSES)]
-        y_first = sbuf("y_first", [P, C], F32)
+        groups = [(0, 1), (1, 2), (2, 4)]
+        y_parts = [sbuf(f"y_part{g}", [P, C * (b - a)], F32) for g, (a, b) in enumerate(groups)]
+        gated = [sbuf(f"gated{g}", [P, C], F32) for g in range(2)]
+        identity = sbuf("identity", [P, P], F32)
+        gate_cols = sbuf("gate_cols", [P, 2], F32)
+        gate_first = sbuf("gate_first", [P, 2 * C], F32)
+        gate_rest = sbuf("gate_rest", [P, 2 * C], F32)
         z_sb = sbuf("z_sb", [P, SLOTS], F32)
-        gate_first = sbuf("gate_first", [P, C], F32)
-        gate_rest = sbuf("gate_rest", [P, 3 * C], F32)
         own = sbuf("own", [P, T], F32)
         warm_in = sbuf("warm_in", [P, 8], F32)
         warm_out = sbuf("warm_out", [P, 8], F32)
-        y_banks = [psum.tile([P, C], F32, name="y_bank_first"), psum.tile([P, 3 * C], F32, name="y_bank_rest")]
+        y_banks = [psum.tile([P, C * (b - a)], F32, name=f"y_bank{g}") for g, (a, b) in enumerate(groups)]
+        gate_bank = psum.tile([P, 2, C], F32, name="gate_bank")
+        z_bank = psum.tile([P, SLOTS], F32, name="z_bank")
 
         xo_rows = xo.rearrange("(s p t) c -> s t p c", s=PASSES, p=P, t=4)
 
         def own_offsets(a, b):
             return own_list[:, a // 16 : b // 16]
 
-        def far_offsets(a, b):
-            return far_list[:, a // 16 : b // 16]
-
         def load_row(j):
             nc.sync.dma_start(out=rows[j], in_=xo_rows[j // 4][j % 4])
 
         def load_pair(i):
             nc.sync.dma_start(out=row_pairs[i][:], in_=xo[: 4 * P].rearrange("(p u e) c -> u p e c", u=2, e=2)[i])
+
+        def load_far_words(s):
+            nc.sync.dma_start(out=far_words[s][:], in_=x_words[s].rearrange("p t d -> p (t d)").bitcast(I32))
 
         def scalar_pick(j, a, b):
             nc.scalar.activation(picked(j // 4, a, b)[:, j % 4, :], rows[j].indirect(own_offsets(a, b)), COPY)
@@ -88,12 +96,9 @@ def tile_moe_loc_lin_gelu_kernel(tc, x_words, x_scales, xo, w_words, w_scales, g
         def weave(s, a, b, count=4):
             nc.vector.tensor_copy(woven[s][:, a:b, :count], picked(s, a, b)[:, :count, :].rearrange("p t c -> p c t"))
 
-        def quantise(s, a, b, tag=None):
-            codes = sbuf(f"own_codes{s}_{a}", [P, b - a], U32, tag=tag)
-            for e in range(a // C, b // C):
-                own_codes[(s, e)] = codes[:, C * e - a : C * (e + 1) - a]
+        def quantise(s, a, b):
             nc.vector.quantize_mx(
-                out=codes[:].bitcast(FP8X4),
+                out=own_codes[s][:, a:b].bitcast(FP8X4),
                 scales=own_scales[s][:, a:b],
                 in_=woven[s][:, a:b, :].rearrange("p c t -> p (c t)"),
             )
@@ -101,29 +106,36 @@ def tile_moe_loc_lin_gelu_kernel(tc, x_words, x_scales, xo, w_words, w_scales, g
         def expert_pass(bank, codes, scales, e, s, start, stop):
             nc.tensor.matmul_mx(
                 out=bank,
-                lhsT=(w_codes[0][:, s, :] if e == 0 else w_codes[1][:, PASSES * (e - 1) + s, :]).bitcast(FP4X4),
+                lhsT=w_codes[e // 2][:, PASSES * (e % 2) + s, :].bitcast(FP4X4),
                 lhsT_scale=w_scale_rows[:, PASSES * e + s, :],
-                rhs=codes.bitcast(FP8X4),
+                rhs=codes[s][:, C * e : C * (e + 1)].bitcast(FP8X4),
                 rhs_scale=scales[s][:, C * e : C * (e + 1)],
                 start=start,
                 stop=stop,
             )
 
-        def own_pass(bank, e, s, start, stop):
-            expert_pass(bank, own_codes[(s, e)], own_scales, e, s, start, stop)
+        def own_group(g):
+            a, b = groups[g]
+            for s in range(PASSES):
+                for e in range(a, b):
+                    expert_pass(y_banks[g][:, C * (e - a) : C * (e - a + 1)], own_codes, own_scales, e, s, (s, e) == (0, a), (s, e) == (1, b - 1))
+            nc.scalar.activation(y_parts[g][:], y_banks[g][:], GELU)
 
-        def load_far_words(s):
-            nc.sync.dma_start(out=far_words[s][:], in_=x_words[s].rearrange("p t d -> p (t d)").bitcast(I32))
+        def scalar_scatter(e):
+            nc.gpsimd.tensor_tensor(gated[e][:], y_parts[e][:], gate_first[:, C * e : C * (e + 1)], MULT)
+            nc.scalar.activation(own[:].indirect(own_offsets(C * e, C * (e + 1))), gated[e][:], COPY)
 
-        def gather_far_words(s, a, b):
-            nc.vector.tensor_copy(far_codes[s][:, a:b], far_words[s][:].bitcast(U32).indirect(far_offsets(a, b)))
-
+        nc.sync.dma_start(out=gate_cols[:], in_=gate[0, : 2 * C].rearrange("(p i) -> p i", i=2))
+        make_identity(nc, identity[:])
         nc.vector.memset(far_scale_rows[:].bitcast(I32), 0)
         nc.vector.memset(warm_in[:], 0.0)
         nc.vector.memset(w_scale_rows[:].rearrange("p g n -> p (g n)").bitcast(I32), 0)
         nc.vector.memset(far_scales[1][:].bitcast(I32), 0)
         nc.vector.memset(own[:], 0.0)
         nc.scalar.activation(warm_out[:], warm_in[:], GELU)
+        for i in range(2):
+            nc.tensor.transpose(gate_bank[:, i, :], gate_cols[:, i : i + 1].to_broadcast([P, P]), identity[:])
+        nc.vector.tensor_copy(gate_first[:].rearrange("p (n i) -> p n i", i=2), gate_bank[:].rearrange("p i n -> p n i"))
 
         load_pair(0)
         nc.sync.dma_start(own_list[:], offs)
@@ -139,12 +151,11 @@ def tile_moe_loc_lin_gelu_kernel(tc, x_words, x_scales, xo, w_words, w_scales, g
         for q in range(1, 4):
             nc.sync.dma_start(out=w_scale_words[32 * q : 32 * q + 4, :], in_=w_scale_words[4 * q : 4 * q + 4, :])
         w_view = w_words.rearrange("e s p b -> p (e s) b").bitcast(I32)
-        nc.sync.dma_start(out=w_codes[0][:].bitcast(I32), in_=w_view[:, :PASSES, :])
+        for h in range(2):
+            nc.sync.dma_start(out=w_codes[h][:].bitcast(I32), in_=w_view[:, 2 * PASSES * h : 2 * PASSES * (h + 1), :])
         load_far_words(0)
-        nc.sync.dma_start(out=gate_first[:], in_=gate[:, :C])
-        nc.sync.dma_start(out=w_codes[1][:].bitcast(I32), in_=w_view[:, PASSES:, :])
         load_far_words(1)
-        nc.sync.dma_start(out=gate_rest[:], in_=gate[:, C:])
+        nc.sync.dma_start(out=gate_rest[:], in_=gate[:, 2 * C :])
 
         scalar_pick(0, 0, SLOTS)
         scalar_pick(1, 0, 2 * C)
@@ -166,36 +177,28 @@ def tile_moe_loc_lin_gelu_kernel(tc, x_words, x_scales, xo, w_words, w_scales, g
         scalar_pick(6, 3 * C, SLOTS)
         vector_pick_woven(6, 0, C)
         weave(1, 0, C, 2)
+
         vector_pick_woven(7, 0, C)
-        vector_pick(7, 3 * C, SLOTS)
-        for e in range(1, 3):
-            scalar_pick(7, C * e, C * (e + 1))
+        scalar_pick(7, C, 2 * C)
+        scalar_pick(7, 3 * C, SLOTS)
+        vector_pick(7, 2 * C, 3 * C)
         nc.scalar.copy(woven[1][:, 3 * C :, :], picked_last[:].rearrange("p t c -> p c t"))
-        own_pass(y_banks[0][:], 0, 0, True, False)
-
         quantise(1, 0, C)
+        own_group(0)
         weave(1, C, 2 * C)
-        own_pass(y_banks[0][:], 0, 1, False, True)
-        nc.scalar.activation(y_first[:], y_banks[0][:], GELU)
         weave(1, 2 * C, 3 * C)
-        quantise(1, C, 2 * C, tag="picked1")
+        quantise(1, C, 2 * C)
+        own_group(1)
+        scalar_scatter(0)
         quantise(1, 2 * C, 4 * C)
-        gated = sbuf("gated", [P, C], F32, tag="picked_last")
-        nc.gpsimd.tensor_tensor(gated[:], y_first[:], gate_first[:], MULT)
-        nc.scalar.activation(own[:].indirect(own_offsets(0, C)), gated[:], COPY)
-        for s in range(PASSES):
-            for e in range(1, E):
-                own_pass(y_banks[1][:, C * (e - 1) : C * e], e, s, (s, e) == (0, 1), (s, e) == (1, E - 1))
-        y_rest = sbuf("y_rest", [P, 3 * C], F32, tag="picked_last")
-        nc.scalar.activation(y_rest[:], y_banks[1][:], GELU)
+        own_group(2)
+        scalar_scatter(1)
 
-        far_codes = [sbuf("far_codes0", [P, SLOTS], U32, tag="woven1"), sbuf("far_codes1", [P, SLOTS], U32)]
-        z_bank = psum.tile([P, SLOTS], F32, name="z_bank")
         for s in range(PASSES):
-            gather_far_words(s, 0, SLOTS)
-            for e in (3, 2, 1, 0):
-                expert_pass(z_bank[:, C * e : C * (e + 1)], far_codes[s][:, C * e : C * (e + 1)], far_scales, e, s, (s, e) == (0, 3), (s, e) == (1, 0))
+            nc.vector.tensor_copy(far_codes[s][:], far_words[s][:].bitcast(U32).indirect(far_list[:]))
+            for e in range(E):
+                expert_pass(z_bank[:, C * e : C * (e + 1)], far_codes, far_scales, e, s, (s, e) == (0, 0), (s, e) == (1, E - 1))
         nc.scalar.activation(z_sb[:], z_bank[:], GELU)
-        nc.vector.tensor_tensor(own[:].indirect(own_offsets(C, SLOTS)), y_rest[:], gate_rest[:], MULT)
+        nc.vector.tensor_tensor(own[:].indirect(own_offsets(2 * C, SLOTS)), y_parts[2][:], gate_rest[:], MULT)
         nc.scalar.dma_start(out=out[:, T:], in_=z_sb[:])
         nc.sync.dma_start(out=out[:, :T], in_=own[:])

@@ -68,7 +68,8 @@ def tile_moe_loc_lin_gelu_kernel(tc, x_words, x_scales, xo, w_words, w_scales, g
         warm_out = sbuf("warm_out", [P, 8], F32)
         y_banks = [psum.tile([P, C * (b - a)], F32, name=f"y_bank{g}") for g, (a, b) in enumerate(groups)]
         gate_bank = psum.tile([P, 2, C], F32, name="gate_bank")
-        z_bank = psum.tile([P, SLOTS], F32, name="z_bank")
+        far_groups = [(0, 2), (2, 4)]
+        z_banks = [psum.tile([P, C * (b - a)], F32, name=f"z_bank{a}") for a, b in far_groups]
 
         xo_rows = xo.rearrange("(s p t) c -> s t p c", s=PASSES, p=P, t=4)
 
@@ -194,11 +195,15 @@ def tile_moe_loc_lin_gelu_kernel(tc, x_words, x_scales, xo, w_words, w_scales, g
         own_group(2)
         scalar_scatter(1)
 
-        for s in range(PASSES):
-            nc.vector.tensor_copy(far_codes[s][:], far_words[s][:].bitcast(U32).indirect(far_list[:]))
-            for e in range(E):
-                expert_pass(z_bank[:, C * e : C * (e + 1)], far_codes, far_scales, e, s, (s, e) == (0, 0), (s, e) == (1, E - 1))
-        nc.scalar.activation(z_sb[:], z_bank[:], GELU)
+        nc.vector.tensor_copy(far_codes[0][:], far_words[0][:].bitcast(U32).indirect(far_list[:]))
+        for g, (a, b) in enumerate(far_groups):
+            for e in range(a, b):
+                expert_pass(z_banks[g][:, C * (e - a) : C * (e - a + 1)], far_codes, far_scales, e, 0, e == a, False)
+        for g, (a, b) in enumerate(far_groups):
+            nc.vector.tensor_copy(far_codes[1][:, C * a : C * b], far_words[1][:].bitcast(U32).indirect(far_list[:, C * a // 16 : C * b // 16]))
+            for e in range(a, b):
+                expert_pass(z_banks[g][:, C * (e - a) : C * (e - a + 1)], far_codes, far_scales, e, 1, False, e == b - 1)
+            nc.scalar.activation(z_sb[:, C * a : C * b], z_banks[g][:], GELU)
         nc.vector.tensor_tensor(own[:].indirect(own_offsets(2 * C, SLOTS)), y_parts[2][:], gate_rest[:], MULT)
         nc.scalar.dma_start(out=out[:, T:], in_=z_sb[:])
         nc.sync.dma_start(out=out[:, :T], in_=own[:])

@@ -59,7 +59,7 @@ def tile_moe_loc_lin_gelu_kernel(tc, x_words, x_scales, xo, w_words, w_scales, g
         y_parts = [sbuf(f"y_part{g}", [P, C * (b - a)], F32) for g, (a, b) in enumerate(groups)]
         gated = [sbuf(f"gated{g}", [P, C], F32) for g in range(2)]
         identity = sbuf("identity", [P, P], F32)
-        gate_cols = sbuf("gate_cols", [P, 2], F32)
+        gate_cols = sbuf("gate_cols", [P, 8], F32)
         gate_first = sbuf("gate_first", [P, 2 * C], F32)
         gate_rest = sbuf("gate_rest", [P, 2 * C], F32)
         z_sb = sbuf("z_sb", [P, SLOTS], F32)
@@ -67,8 +67,8 @@ def tile_moe_loc_lin_gelu_kernel(tc, x_words, x_scales, xo, w_words, w_scales, g
         warm_in = sbuf("warm_in", [P, 8], F32)
         warm_out = sbuf("warm_out", [P, 8], F32)
         y_banks = [psum.tile([P, C * (b - a)], F32, name=f"y_bank{g}") for g, (a, b) in enumerate(groups)]
-        gate_bank = psum.tile([P, 2, C], F32, name="gate_bank")
-        far_groups = [(0, 2), (2, 4)]
+        gate_banks = [psum.tile([P, 4, P], F32, name=f"gate_bank{h}") for h in range(2)]
+        far_groups = [(0, 2), (2, 3), (3, 4)]
         z_banks = [psum.tile([P, C * (b - a)], F32, name=f"z_bank{a}") for a, b in far_groups]
 
         xo_rows = xo.rearrange("(s p t) c -> s t p c", s=PASSES, p=P, t=4)
@@ -126,7 +126,9 @@ def tile_moe_loc_lin_gelu_kernel(tc, x_words, x_scales, xo, w_words, w_scales, g
             nc.gpsimd.tensor_tensor(gated[e][:], y_parts[e][:], gate_first[:, C * e : C * (e + 1)], MULT)
             nc.scalar.activation(own[:].indirect(own_offsets(C * e, C * (e + 1))), gated[e][:], COPY)
 
-        nc.sync.dma_start(out=gate_cols[:], in_=gate[0, : 2 * C].rearrange("(p i) -> p i", i=2))
+        nc.sync.dma_start(out=gate_cols[:32, :], in_=gate[0, : 2 * C].rearrange("(p i) -> p i", i=8))
+        nc.gpsimd.memset(gate_cols[32:64, :], 0.0)
+        nc.gpsimd.memset(gate_cols[64:, :], 0.0)
         make_identity(nc, identity[:])
         nc.vector.memset(far_scale_rows[:].bitcast(I32), 0)
         nc.vector.memset(warm_in[:], 0.0)
@@ -134,9 +136,10 @@ def tile_moe_loc_lin_gelu_kernel(tc, x_words, x_scales, xo, w_words, w_scales, g
         nc.vector.memset(far_scales[1][:].bitcast(I32), 0)
         nc.vector.memset(own[:], 0.0)
         nc.scalar.activation(warm_out[:], warm_in[:], GELU)
-        for i in range(2):
-            nc.tensor.transpose(gate_bank[:, i, :], gate_cols[:, i : i + 1].to_broadcast([P, P]), identity[:])
-        nc.vector.tensor_copy(gate_first[:].rearrange("p (n i) -> p n i", i=2), gate_bank[:].rearrange("p i n -> p n i"))
+        for h in range(2):
+            for i in range(4):
+                nc.tensor.transpose(gate_banks[h][:, i, :], gate_cols[:, 4 * h + i : 4 * h + i + 1].to_broadcast([P, P]), identity[:])
+            nc.vector.tensor_copy(gate_first[:].rearrange("p (n h i) -> p h n i", h=2, i=4)[:, h], gate_banks[h][:, :, :32].rearrange("p i n -> p n i"))
 
         load_pair(0)
         nc.sync.dma_start(own_list[:], offs)
@@ -205,5 +208,6 @@ def tile_moe_loc_lin_gelu_kernel(tc, x_words, x_scales, xo, w_words, w_scales, g
                 expert_pass(z_banks[g][:, C * (e - a) : C * (e - a + 1)], far_codes, far_scales, e, 1, False, e == b - 1)
             nc.scalar.activation(z_sb[:, C * a : C * b], z_banks[g][:], GELU)
         nc.vector.tensor_tensor(own[:].indirect(own_offsets(2 * C, SLOTS)), y_parts[2][:], gate_rest[:], MULT)
-        nc.scalar.dma_start(out=out[:, T:], in_=z_sb[:])
+        nc.scalar.dma_start(out=out[:, T : T + 2 * C], in_=z_sb[:, : 2 * C])
+        nc.scalar.dma_start(out=out[:, T + 2 * C :], in_=z_sb[:, 2 * C :])
         nc.sync.dma_start(out=out[:, :T], in_=own[:])

@@ -148,12 +148,11 @@ def tile_moe_loc_lin_gelu_kernel(tc, x_words, x_scales, xo, w_words, w_scales, g
         for r in range(4):
             nc.sync.dma_start(out=far_scale_rows[r:P:16, :].bitcast(I32), in_=x_rows[r].bitcast(I32))
         load_pair(1)
-        nc.sync.dma_start(out=w_scale_rows[:16, :, :].bitcast(I32), in_=w_scales.rearrange("e s b n -> b (e s) n").bitcast(I32))
         for j in range(4, 8):
             load_row(j)
-        w_scale_words = w_scale_rows[:].rearrange("p g n -> p (g n)").bitcast(I32)
-        for q in range(1, 4):
-            nc.sync.dma_start(out=w_scale_words[32 * q : 32 * q + 4, :], in_=w_scale_words[4 * q : 4 * q + 4, :])
+        w_rows = w_scales.rearrange("e s (q r) n -> r q (e s) n", r=4)
+        for r in range(4):
+            nc.sync.dma_start(out=w_scale_rows[r:P:32, :, :].bitcast(I32), in_=w_rows[r].bitcast(I32))
         w_view = w_words.rearrange("e s p b -> p (e s) b").bitcast(I32)
         for h in range(2):
             nc.sync.dma_start(out=w_codes[h][:].bitcast(I32), in_=w_view[:, 2 * PASSES * h : 2 * PASSES * (h + 1), :])

@@ -123,7 +123,7 @@ def tile_moe_loc_lin_gelu_kernel(tc, x_words, x_scales, xo, w_words, w_scales, g
             nc.scalar.activation(y_parts[g][:], y_banks[g][:], GELU)
 
         def scalar_scatter(e):
-            nc.gpsimd.tensor_tensor(gated[e][:], y_parts[e][:], gate_first[:, C * e : C * (e + 1)], MULT)
+            (nc.vector if e == 0 else nc.gpsimd).tensor_tensor(gated[e][:], y_parts[e][:], gate_first[:, C * e : C * (e + 1)], MULT)
             nc.scalar.activation(own[:].indirect(own_offsets(C * e, C * (e + 1))), gated[e][:], COPY)
 
         nc.sync.dma_start(out=gate_cols[:32, :], in_=gate[0, : 2 * C].rearrange("(p i) -> p i", i=8))
@@ -192,8 +192,8 @@ def tile_moe_loc_lin_gelu_kernel(tc, x_words, x_scales, xo, w_words, w_scales, g
         weave(1, 2 * C, 3 * C)
         quantise(1, C, 2 * C)
         own_group(1)
-        scalar_scatter(0)
         quantise(1, 2 * C, 4 * C)
+        scalar_scatter(0)
         own_group(2)
         scalar_scatter(1)
 

@@ -31,7 +31,7 @@ def tile_moe_loc_lin_gelu_kernel(tc, x_words, x_scales, xo, w_words, w_scales, g
         psum = ctx.enter_context(tc.psum_pool(name="psum", bufs=1))
 
         def sbuf(name, shape, dtype, tag=None):
-            return keep.tile(shape, dtype, name=name, tag=tag or name, align_bytes=64)
+            return keep.tile(shape, dtype, name=name, tag=tag or name, align_bytes=256)
 
         own_list = keep.tile([P, LIST_COLS], U16, name="own_list")
         far_list = keep.tile([P, LIST_COLS], U16, name="far_list")

@@ -59,15 +59,16 @@ def tile_moe_loc_lin_gelu_kernel(tc, x_words, x_scales, xo, w_words, w_scales, g
         y_parts = [sbuf(f"y_part{g}", [P, C * (b - a)], F32) for g, (a, b) in enumerate(groups)]
         gated = [sbuf(f"gated{g}", [P, C], F32) for g in range(2)]
         identity = sbuf("identity", [P, P], F32)
-        gate_cols = sbuf("gate_cols", [P, 8], F32)
-        gate_first = sbuf("gate_first", [P, 2 * C], F32)
+        gate_cols = sbuf("gate_cols", [P, 2], F32)
+        gate_one = sbuf("gate_one", [P, C], F32)
         gate_rest = sbuf("gate_rest", [P, 2 * C], F32)
         z_sb = sbuf("z_sb", [P, SLOTS], F32)
         own = sbuf("own", [P, T], F32)
         warm_in = sbuf("warm_in", [P, 8], F32)
         warm_out = sbuf("warm_out", [P, 8], F32)
         y_banks = [psum.tile([P, C * (b - a)], F32, name=f"y_bank{g}") for g, (a, b) in enumerate(groups)]
-        gate_banks = [psum.tile([P, 4, P], F32, name=f"gate_bank{h}") for h in range(2)]
+        gate_bank = psum.tile([P, 2, P], F32, name="gate_bank")
+        gate_slots = gate_bank[:].rearrange("p i n -> p n i")
         far_groups = [(0, 2), (2, 3), (3, 4)]
         z_banks = [psum.tile([P, C * (b - a)], F32, name=f"z_bank{a}") for a, b in far_groups]
 
@@ -123,12 +124,12 @@ def tile_moe_loc_lin_gelu_kernel(tc, x_words, x_scales, xo, w_words, w_scales, g
             nc.scalar.activation(y_parts[g][:], y_banks[g][:], GELU)
 
         def scalar_scatter(e):
-            (nc.vector if e == 0 else nc.gpsimd).tensor_tensor(gated[e][:], y_parts[e][:], gate_first[:, C * e : C * (e + 1)], MULT)
+            if e == 0:
+                nc.vector.tensor_tensor(gated[e][:].rearrange("p (n i) -> p n i", i=2), y_parts[e][:].rearrange("p (n i) -> p n i", i=2), gate_slots[:, : C // 2, :], MULT)
+            else:
+                nc.gpsimd.tensor_tensor(gated[e][:], y_parts[e][:], gate_one[:], MULT)
             nc.scalar.activation(own[:].indirect(own_offsets(C * e, C * (e + 1))), gated[e][:], COPY)
 
-        nc.sync.dma_start(out=gate_cols[:32, :], in_=gate[0, : 2 * C].rearrange("(p i) -> p i", i=8))
-        nc.gpsimd.memset(gate_cols[32:64, :], 0.0)
-        nc.gpsimd.memset(gate_cols[64:, :], 0.0)
         make_identity(nc, identity[:])
         nc.vector.memset(far_scale_rows[:].bitcast(I32), 0)
         nc.vector.memset(warm_in[:], 0.0)
@@ -136,10 +137,6 @@ def tile_moe_loc_lin_gelu_kernel(tc, x_words, x_scales, xo, w_words, w_scales, g
         nc.vector.memset(far_scales[1][:].bitcast(I32), 0)
         nc.vector.memset(own[:], 0.0)
         nc.scalar.activation(warm_out[:], warm_in[:], GELU)
-        for h in range(2):
-            for i in range(4):
-                nc.tensor.transpose(gate_banks[h][:, i, :], gate_cols[:, 4 * h + i : 4 * h + i + 1].to_broadcast([P, P]), identity[:])
-            nc.vector.tensor_copy(gate_first[:].rearrange("p (n h i) -> p h n i", h=2, i=4)[:, h], gate_banks[h][:, :, :32].rearrange("p i n -> p n i"))
 
         load_pair(0)
         nc.sync.dma_start(own_list[:], offs)
@@ -148,6 +145,7 @@ def tile_moe_loc_lin_gelu_kernel(tc, x_words, x_scales, xo, w_words, w_scales, g
         for r in range(4):
             nc.sync.dma_start(out=far_scale_rows[r:P:16, :].bitcast(I32), in_=x_rows[r].bitcast(I32))
         load_pair(1)
+        nc.sync.dma_start(out=gate_cols[:], in_=gate[0, : 2 * C].rearrange("(p i) -> p i", i=2))
         for j in range(4, 8):
             load_row(j)
         w_rows = w_scales.rearrange("e s (q r) n -> r q (e s) n", r=4)
@@ -176,6 +174,9 @@ def tile_moe_loc_lin_gelu_kernel(tc, x_words, x_scales, xo, w_words, w_scales, g
         scalar_pick(4, 3 * C, SLOTS)
         scalar_pick(5, 0, 3 * C)
         vector_pick(5, 3 * C, SLOTS)
+        for i in range(2):
+            nc.tensor.transpose(gate_bank[:, i, :], gate_cols[:, i : i + 1].to_broadcast([P, P]), identity[:])
+        nc.scalar.copy(gate_one[:].rearrange("p (n i) -> p n i", i=2), gate_slots[:, C // 2 :, :])
         scalar_pick(6, C, 3 * C)
         scalar_pick(6, 3 * C, SLOTS)
         vector_pick_woven(6, 0, C)

@@ -22,6 +22,7 @@ FP4X4 = mybir.dt.float4_e2m1fn_x4
 GELU = mybir.ActivationFunctionType.Gelu_apprx_tanh
 COPY = mybir.ActivationFunctionType.Copy
 MULT = mybir.AluOpType.mult
+ADD = mybir.AluOpType.add
 
 
 def tile_moe_loc_lin_gelu_kernel(tc, x_words, x_scales, xo, w_words, w_scales, gate, offs, offs2, out):
@@ -163,13 +164,14 @@ def tile_moe_loc_lin_gelu_kernel(tc, x_words, x_scales, xo, w_words, w_scales, g
         vector_pick(1, 2 * C, SLOTS)
         nc.vector.tensor_copy(far_scales[0][:], far_scale_rows[:].indirect(far_list[:]))
         nc.sync.dma_start(out=far_scales[1][0 : P - 16, :].bitcast(I32), in_=far_scales[0][16:P, :].bitcast(I32))
-        for h in range(2):
-            scalar_pick(2, 2 * C * h, 2 * C * (h + 1))
-            vector_pick(3, 2 * C * h, 2 * C * (h + 1))
-        for h in range(2):
-            weave(0, 2 * C * h, 2 * C * (h + 1))
-        for h in range(2):
-            quantise(0, 2 * C * h, 2 * C * (h + 1))
+        for a, b in ((0, C), (C, SLOTS)):
+            scalar_pick(2, a, b)
+            vector_pick(3, a, b)
+        nc.gpsimd.tensor_scalar(woven[0][:, :C, :], picked0[:, :, :C].rearrange("p t c -> p c t"), 1.0, 0.0, MULT, ADD)
+        weave(0, 2 * C, SLOTS)
+        weave(0, C, 2 * C)
+        quantise(0, 2 * C, SLOTS)
+        quantise(0, 0, 2 * C)
         scalar_pick(4, 0, 3 * C)
         scalar_pick(4, 3 * C, SLOTS)
         scalar_pick(5, 0, 3 * C)

from contextlib import ExitStack

import concourse.mybir as mybir
from concourse.masks import make_identity

K, T, Q, E, C, N = 1024, 1024, 1024, 4, 128, 128
P = 128
PASSES = 2
SLOTS = E * C
LIST_COLS = SLOTS // 16

FLOPS = 2 * K * N * 2 * SLOTS

F32 = mybir.dt.float32
BF16 = mybir.dt.bfloat16
I32 = mybir.dt.int32
U32 = mybir.dt.uint32
U16 = mybir.dt.uint16
U8 = mybir.dt.uint8
FP8X4 = mybir.dt.float8_e4m3fn_x4
FP4X4 = mybir.dt.float4_e2m1fn_x4
GELU = mybir.ActivationFunctionType.Gelu_apprx_tanh
COPY = mybir.ActivationFunctionType.Copy
MULT = mybir.AluOpType.mult
ADD = mybir.AluOpType.add


def tile_moe_loc_lin_gelu_kernel(tc, x_words, x_scales, xo, w_words, w_scales, gate, offs, offs2, out):
    nc = tc.nc
    with ExitStack() as ctx:
        keep = ctx.enter_context(tc.tile_pool(name="keep", bufs=1))
        psum = ctx.enter_context(tc.psum_pool(name="psum", bufs=1))

        def sbuf(name, shape, dtype, tag=None):
            return keep.tile(shape, dtype, name=name, tag=tag or name, align_bytes=256)

        own_list = keep.tile([P, LIST_COLS], U16, name="own_list")
        far_list = keep.tile([P, LIST_COLS], U16, name="far_list")
        far_scale_rows = sbuf("far_scale_rows", [P, Q], U8)
        w_scale_rows = sbuf("w_scale_rows", [P, E * PASSES, N], U8)
        w_codes = [sbuf(f"w_half{h}", [P, 2 * PASSES, 2 * N], U8) for h in range(2)]
        far_words = [sbuf(f"far_words{s}", [P, Q], I32) for s in range(PASSES)]
        far_scales = [sbuf(f"far_scales{s}", [P, SLOTS], U8) for s in range(PASSES)]
        far_codes = [sbuf(f"far_codes{s}", [P, SLOTS], U32) for s in range(PASSES)]
        row_pairs = [sbuf(f"row_pair{i}", [P, 2, T], F32) for i in range(2)]
        rows = [row_pairs[j // 2][:, j % 2, :] for j in range(4)] + [sbuf(f"row{j}", [P, T], F32)[:] for j in range(4, 8)]
        picked0 = sbuf("picked0", [P, 4, SLOTS], F32)
        picked1 = sbuf("picked1", [P, 4, 3 * C], BF16)
        picked_last = sbuf("picked_last", [P, 4, C], BF16)

        def picked(s, a, b):
            if s == 0:
                return picked0[:, :, a:b]
            return picked1[:, :, a:b] if a < 3 * C else picked_last[:, :, a - 3 * C : b - 3 * C]

        woven = [sbuf(f"woven{s}", [P, SLOTS, 4], BF16) for s in range(PASSES)]
        own_codes = [sbuf(f"own_codes{s}", [P, SLOTS], U32) for s in range(PASSES)]
        own_scales = [sbuf(f"own_scales{s}", [P, SLOTS], U8) for s in range(PASSES)]
        groups = [(0, 1), (1, 2), (2, 4)]
        y_parts = [sbuf(f"y_part{g}", [P, C * (b - a)], F32) for g, (a, b) in enumerate(groups)]
        gated = [sbuf(f"gated{g}", [P, C], F32) for g in range(2)]
        identity = sbuf("identity", [P, P], F32)
        gate_cols = sbuf("gate_cols", [P, 2], F32)
        gate_one = sbuf("gate_one", [P, C], F32)
        gate_rest = sbuf("gate_rest", [P, 2 * C], F32)
        z_sb = sbuf("z_sb", [P, SLOTS], F32)
        own = sbuf("own", [P, T], F32)
        warm_in = sbuf("warm_in", [P, 8], F32)
        warm_out = sbuf("warm_out", [P, 8], F32)
        y_banks = [psum.tile([P, C * (b - a)], F32, name=f"y_bank{g}") for g, (a, b) in enumerate(groups)]
        gate_bank = psum.tile([P, 2, P], F32, name="gate_bank")
        gate_slots = gate_bank[:].rearrange("p i n -> p n i")
        far_groups = [(0, 2), (2, 3), (3, 4)]
        z_banks = [psum.tile([P, C * (b - a)], F32, name=f"z_bank{a}") for a, b in far_groups]

        xo_rows = xo.rearrange("(s p t) c -> s t p c", s=PASSES, p=P, t=4)

        def own_offsets(a, b):
            return own_list[:, a // 16 : b // 16]

        def load_row(j):
            nc.sync.dma_start(out=rows[j], in_=xo_rows[j // 4][j % 4])

        def load_pair(i):
            nc.sync.dma_start(out=row_pairs[i][:], in_=xo[: 4 * P].rearrange("(p u e) c -> u p e c", u=2, e=2)[i])

        def load_far_words(s):
            nc.sync.dma_start(out=far_words[s][:], in_=x_words[s].rearrange("p t d -> p (t d)").bitcast(I32))

        def scalar_pick(j, a, b):
            nc.scalar.activation(picked(j // 4, a, b)[:, j % 4, :], rows[j].indirect(own_offsets(a, b)), COPY)

        def vector_pick(j, a, b):
            nc.vector.tensor_copy(picked(j // 4, a, b)[:, j % 4, :], rows[j].indirect(own_offsets(a, b)))

        def vector_pick_woven(j, a, b):
            nc.vector.tensor_copy(woven[j // 4][:, a:b, j % 4], rows[j].indirect(own_offsets(a, b)))

        def weave(s, a, b, count=4):
            nc.vector.tensor_copy(woven[s][:, a:b, :count], picked(s, a, b)[:, :count, :].rearrange("p t c -> p c t"))

        def quantise(s, a, b):
            nc.vector.quantize_mx(
                out=own_codes[s][:, a:b].bitcast(FP8X4),
                scales=own_scales[s][:, a:b],
                in_=woven[s][:, a:b, :].rearrange("p c t -> p (c t)"),
            )

        def expert_pass(bank, codes, scales, e, s, start, stop):
            nc.tensor.matmul_mx(
                out=bank,
                lhsT=w_codes[e // 2][:, PASSES * (e % 2) + s, :].bitcast(FP4X4),
                lhsT_scale=w_scale_rows[:, PASSES * e + s, :],
                rhs=codes[s][:, C * e : C * (e + 1)].bitcast(FP8X4),
                rhs_scale=scales[s][:, C * e : C * (e + 1)],
                start=start,
                stop=stop,
            )

        def own_group(g):
            a, b = groups[g]
            for s in range(PASSES):
                for e in range(a, b):
                    expert_pass(y_banks[g][:, C * (e - a) : C * (e - a + 1)], own_codes, own_scales, e, s, (s, e) == (0, a), (s, e) == (1, b - 1))
            nc.scalar.activation(y_parts[g][:], y_banks[g][:], GELU)

        def scalar_scatter(e):
            if e == 0:
                nc.vector.tensor_tensor(gated[e][:].rearrange("p (n i) -> p n i", i=2), y_parts[e][:].rearrange("p (n i) -> p n i", i=2), gate_slots[:, : C // 2, :], MULT)
            else:
                nc.gpsimd.tensor_tensor(gated[e][:], y_parts[e][:], gate_one[:], MULT)
            nc.scalar.activation(own[:].indirect(own_offsets(C * e, C * (e + 1))), gated[e][:], COPY)

        make_identity(nc, identity[:])
        nc.vector.memset(far_scale_rows[:].bitcast(I32), 0)
        nc.vector.memset(warm_in[:], 0.0)
        nc.vector.memset(w_scale_rows[:].rearrange("p g n -> p (g n)").bitcast(I32), 0)
        nc.vector.memset(far_scales[1][:].bitcast(I32), 0)
        nc.vector.memset(own[:], 0.0)
        nc.scalar.activation(warm_out[:], warm_in[:], GELU)

        load_pair(0)
        nc.sync.dma_start(own_list[:], offs)
        nc.sync.dma_start(far_list[:], offs2)
        x_rows = x_scales.rearrange("s (q r) t -> r q s t", r=4)
        for r in range(4):
            nc.sync.dma_start(out=far_scale_rows[r:P:16, :].bitcast(I32), in_=x_rows[r].bitcast(I32))
        load_pair(1)
        nc.sync.dma_start(out=gate_cols[:], in_=gate[0, : 2 * C].rearrange("(p i) -> p i", i=2))
        for j in range(4, 8):
            load_row(j)
        w_rows = w_scales.rearrange("e s (q r) n -> r q (e s) n", r=4)
        for r in range(4):
            nc.sync.dma_start(out=w_scale_rows[r:P:32, :, :].bitcast(I32), in_=w_rows[r].bitcast(I32))
        w_view = w_words.rearrange("e s p b -> p (e s) b").bitcast(I32)
        for h in range(2):
            nc.sync.dma_start(out=w_codes[h][:].bitcast(I32), in_=w_view[:, 2 * PASSES * h : 2 * PASSES * (h + 1), :])
        load_far_words(0)
        load_far_words(1)
        nc.sync.dma_start(out=gate_rest[:], in_=gate[:, 2 * C :])

        scalar_pick(0, 0, SLOTS)
        scalar_pick(1, 0, 2 * C)
        vector_pick(1, 2 * C, SLOTS)
        nc.vector.tensor_copy(far_scales[0][:], far_scale_rows[:].indirect(far_list[:]))
        nc.sync.dma_start(out=far_scales[1][0 : P - 16, :].bitcast(I32), in_=far_scales[0][16:P, :].bitcast(I32))
        for a, b in ((0, C), (C, SLOTS)):
            scalar_pick(2, a, b)
            vector_pick(3, a, b)
        nc.gpsimd.tensor_scalar(woven[0][:, :C, :], picked0[:, :, :C].rearrange("p t c -> p c t"), 1.0, 0.0, MULT, ADD)
        weave(0, 2 * C, SLOTS)
        weave(0, C, 2 * C)
        quantise(0, 2 * C, SLOTS)
        quantise(0, 0, 2 * C)
        scalar_pick(4, 0, 3 * C)
        scalar_pick(4, 3 * C, SLOTS)
        scalar_pick(5, 0, 3 * C)
        vector_pick(5, 3 * C, SLOTS)
        for i in range(2):
            nc.tensor.transpose(gate_bank[:, i, :], gate_cols[:, i : i + 1].to_broadcast([P, P]), identity[:])
        nc.scalar.copy(gate_one[:].rearrange("p (n i) -> p n i", i=2), gate_slots[:, C // 2 :, :])
        scalar_pick(6, C, 3 * C)
        scalar_pick(6, 3 * C, SLOTS)
        vector_pick_woven(6, 0, C)
        weave(1, 0, C, 2)

        vector_pick_woven(7, 0, C)
        scalar_pick(7, C, 2 * C)
        scalar_pick(7, 3 * C, SLOTS)
        vector_pick(7, 2 * C, 3 * C)
        nc.scalar.copy(woven[1][:, 3 * C :, :], picked_last[:].rearrange("p t c -> p c t"))
        quantise(1, 0, C)
        own_group(0)
        weave(1, C, 2 * C)
        weave(1, 2 * C, 3 * C)
        quantise(1, C, 2 * C)
        own_group(1)
        quantise(1, 2 * C, 4 * C)
        scalar_scatter(0)
        own_group(2)
        scalar_scatter(1)

        nc.vector.tensor_copy(far_codes[0][:], far_words[0][:].bitcast(U32).indirect(far_list[:]))
        for g, (a, b) in enumerate(far_groups):
            for e in range(a, b):
                expert_pass(z_banks[g][:, C * (e - a) : C * (e - a + 1)], far_codes, far_scales, e, 0, e == a, False)
        for g, (a, b) in enumerate(far_groups):
            nc.vector.tensor_copy(far_codes[1][:, C * a : C * b], far_words[1][:].bitcast(U32).indirect(far_list[:, C * a // 16 : C * b // 16]))
            for e in range(a, b):
                expert_pass(z_banks[g][:, C * (e - a) : C * (e - a + 1)], far_codes, far_scales, e, 1, False, e == b - 1)
            nc.scalar.activation(z_sb[:, C * a : C * b], z_banks[g][:], GELU)
        nc.vector.tensor_tensor(own[:].indirect(own_offsets(2 * C, SLOTS)), y_parts[2][:], gate_rest[:], MULT)
        nc.scalar.dma_start(out=out[:, T : T + 2 * C], in_=z_sb[:, : 2 * C])
        nc.scalar.dma_start(out=out[:, T + 2 * C :], in_=z_sb[:, 2 * C :])
        nc.sync.dma_start(out=out[:, :T], in_=own[:])
